import numpy as np, ml_dtypes
CORES = [22,46,70,150,174,198,278,302,326,406,430,454]
N = 12
T, KB = 2048, 64
CAPP = 512
def entries(a): return a.T.reshape(-1)
def pack(v, P): return np.ascontiguousarray(np.asarray(v, np.int32).reshape(-1, P).T)
def order(K):
    return np.argsort(K, kind="stable")
def most(K):
    o = order(K); return int(np.bincount(o // T * N + np.arange(N * T) // T, minlength=N * N).max())
def lists(rng, how):
    i, G = np.arange(N), T // CAPP
    if how == "uniform":
        for again in range(50):
            K = rng.integers(0, KB, (N, T))
            if most(K.reshape(-1)) <= CAPP: break
        else: K = np.broadcast_to(np.arange(T) % KB, (N, T)).copy()
    else:
        if how == "uneven":
            t = rng.integers(0, CAPP + 1, N)
            if t.sum() < T: t = CAPP - t
            t[0] = CAPP; w = np.diff(np.minimum(np.cumsum(t), T), prepend=0); L = w[(rng.permutation(N)[:, None] - rng.permutation(N)) % N]
        else:
            w = np.zeros(N, int); w[(G * (ord(how[-1]) - 97) + np.arange(G)) % N] = CAPP; L = w[(i[:, None] - i) % N]
        a = N - 1 - np.argmax(L[::-1] > 0, axis=0)
        m = np.minimum(rng.integers(1, CAPP, N - 1), L[a[:-1], i[1:]])
        v = np.nonzero((L[a[:-1], i[:-1]] == CAPP) & (L[a[:-1], i[1:]] == CAPP) & (a[:-1] != np.append(-1, a[:-2])))[0]
        if len(v): m[rng.choice(v)] = CAPP
        C = L.copy(); C[a[:-1], i[:-1]] += m; C[a[:-1], i[1:]] -= m
        kv = np.sort(rng.permutation(KB)[:N]); K = np.stack([rng.permutation(np.repeat(kv, c)) for c in C]); K[::3] = np.sort(K[::3], axis=1)
    return {"key": np.stack([pack(k, 16) for k in K])}
def setup_inputs(rng):
    return dict({"x": rng.standard_normal((N, 128, T), dtype=np.float32).astype(ml_dtypes.bfloat16)}, **lists(rng, "uniform"))
def setup_inputs_fulla(rng):
    d = setup_inputs(rng); d.update(lists(rng, "fulla"))
    for k in ("x",): d[k] = (d[k].astype(np.float32) * 1048576.0).astype(d[k].dtype)
    return d
def setup_inputs_fullb(rng):
    d = setup_inputs(rng); d.update(lists(rng, "fullb"))
    for k in ("x",): d[k] = (d[k].astype(np.float32) * (1 / 1024.0)).astype(d[k].dtype)
    return d
def setup_inputs_fullc(rng):
    d = setup_inputs(rng); d.update(lists(rng, "fullc"))
    return d
def setup_inputs_uneven(rng):
    d = setup_inputs(rng); d.update(lists(rng, "uneven"))
    return d
def check_inputs(x):
    bad = []
    if x["key"].min() < 0 or x["key"].max() >= KB: bad.append("key out of range")
    if most(np.concatenate([entries(a) for a in x["key"]])) > CAPP: bad.append("more than CAPP columns go from one rank to one rank")
    return bad
def reference(x, key):
    X = np.concatenate(list(x), axis=1); K = np.concatenate([entries(a) for a in key])
    Y = X[:, order(K)]
    return {"y": np.stack([Y[:, T * r:T * r + T] for r in range(N)])}

@@ -1,0 +1,330 @@
+from concourse.bass import DstId, RemoteDMATransfer
+from concourse.mybir import AluOpType as A, ActivationFunctionType as F
+
+N, W, CAP, H, NE = 12, 2048, 512, 1024, 95
+SMALL = {}
+for _n, _w in (("a1", 12), ("a2", 12), ("a3", 12), ("m1", 12), ("m2", 12), ("zc", 12), ("zm", 12), ("cst", 8), ("wt", 8),
+               ("bcol", 4), ("zo", 8), ("zp", 8), ("p16", 4), ("kcol", 4), ("vcol", 4), ("pmi", 16), ("jc", 16), ("tf", 32),
+               ("rcum", 16), ("dp", 8), ("z", 16), ("bf", 12)):
+    SMALL[_n] = (sum(w for o, w in SMALL.values()), _w)
+SCRATCH = {"hland": ("dram", [12, 128, 1], "float32")}
+for _t, _l in (("float32", "small=%d hrow=128 q0=128 qi=128 c2=128 sx=128 ones=128 neg=128 l2=768 r1=768 r2=768 of=128"
+                % sum(w for o, w in SMALL.values())),
+               ("bfloat16", "kb=64 hv=128 km=128 mv=128 rsl=2048 hself=2 imod=128 cpat=128 xin=2048 xs=2560 snd=3072 land=6144 yb=2048"),
+               ("float16", "oh=1024 prod=1024 tot=1 fold=128 mb=128 hsel=2 hb=2 la=2048 ra=2048"),
+               ("int32", "kraw=64 ti=16 tci=32 pci=1 pai=1 bq=6 bci=12"), ("uint16", "plist=128 wl=192 yoff=128")):
+    for _b in _l.split():
+        SCRATCH[_b.split("=")[0]] = ("sbuf", [128, int(_b.split("=")[1])], _t)
+for _b, _w in (("kps", 1024), ("sps", 1024), ("tps", 512), ("hps", 512), ("pps", 512), ("sts", 512)):
+    SCRATCH[_b] = ("psum", [128, _w], "float32")
+SEMAPHORES = ["e%d" % i for i in range(NE)] + ["xa", "pa", "hd", "hc", "hr", "da", "sent"]
+PLANS = {}
+
+
+def plan(topo, cores):
+    if "p" in PLANS:
+        return PLANS["p"]
+    rk = [topo.rack(topo.host(c)) for c in cores]
+    p = {"partner": [], "twin": [], "rack": [[q for q in range(N) if rk[q] == rk[r]] for r in range(N)]}
+    for r, c in enumerate(cores):
+        s = [q for q in range(N) if rk[q] != rk[r] and topo.chip(cores[q]) == topo.chip(c) and topo.may_write(c, cores[q])][0]
+        d = cores[s]
+        p["partner"].append(s)
+        p["twin"].append([k for k in range(512) if topo.host(k) == topo.host(d) and topo.chip(k) == topo.chip(d) and
+                          topo.die(k) != topo.die(d) and all(topo.may_write(k, cores[q]) for q in p["rack"][s])][0])
+    PLANS["p"] = p
+    return p
+
+
+def engines(mask):
+    return [1 << i for i in range(16) if mask >> i & 1]
+
+
+def send_mask(topo, src, dst, far):
+    m = topo.mask(src, dst)
+    off = topo.mask(src, far)
+    return m & ~off if m & ~off else m
+
+
+def grp():
+    return {"n": 0, "w": False, "sem": None, "cl": set(), "key": None}
+
+
+def run(ops, qs, T):
+    know, ns = {q: set() for q in qs}, 0
+    for num, (q, f, kw, deps, G, n) in enumerate(ops):
+        for d in deps:
+            if isinstance(d, tuple):
+                if d not in know[q]:
+                    qs[q].wait_ge(T.sem[d[0]], d[1])
+                    know[q].add(d)
+            elif d["key"] not in know[q]:
+                qs[q].wait_ge(T.sem["e%d" % d["sem"]], d["n"])
+                know[q] |= d["cl"] | {d["key"]}
+        if f is None:
+            continue
+        if G["key"] is None:
+            G["key"] = num
+            if G["w"]:
+                G["sem"] = ns
+                ns += 1
+        G["cl"] |= know[q]
+        i = f(**kw)
+        if G["w"]:
+            i.then_inc(T.sem["e%d" % G["sem"]], n)
+
+
+def rank_program(g, core, T, topo):
+    P = plan(topo, T.cores)
+    r = T.rank_of(core)
+    if r is not None:
+        body(g, core, T, topo, P, r, True)
+    elif core in P["twin"]:
+        body(g, core, T, topo, P, P["twin"].index(core), False)
+
+
+def body(g, core, T, topo, P, r, is_rank):
+    cores, partner, twin = T.cores, P["partner"], P["twin"]
+    vec, act = g.vector, g.scalar
+    home = r if is_rank else partner[r]
+    mine = P["rack"][home]
+    rtw = [twin[partner[s]] for s in mine]
+    idx = mine.index(home)
+    near = [cores[s] for s in mine if s != home]
+    ops, sent = [], [0]
+
+    def add(q, f, kw, deps=(), G=None, n=1):
+        G = grp() if G is None else G
+        G["n"] += n
+        for d in deps:
+            if not isinstance(d, tuple):
+                d["w"] = True
+        ops.append((q, f, kw, list(deps), G, n))
+        return G
+
+    def S(name, p0=0, p1=128, a=0, b=None):
+        o, w = SMALL[name]
+        return T.small[p0:p1, o + a:o + (w if b is None else b)]
+
+    def ts(out, in0, s1, op0, deps, s2=None, op1=None, G=None):
+        kw = dict(out=out, in0=in0, scalar1=s1, scalar2=s2, op0=op0)
+        if op1 is not None:
+            kw["op1"] = op1
+        return add("v", vec.tensor_scalar, kw, deps, G)
+
+    def tt(out, a, b, op, deps, G=None):
+        return add("v", vec.tensor_tensor, dict(out=out, in0=a, in1=b, op=op), deps, G)
+
+    def scan(out, d, deps, G=None):
+        return add("v", vec.tensor_tensor_scan, dict(out=out, data0=d, data1=d, initial=0.0, op0=A.add, op1=A.max), deps, G)
+
+    def fill(ap, c, G=None, deps=()):
+        return add("v", vec.memset, dict(ap=ap, constant=c), deps, G)
+
+    def cp(out, in_, deps, G=None, q="v"):
+        if q == "v":
+            return add("v", vec.tensor_copy, dict(out=out, in_=in_), deps, G)
+        return add("s", act.activation, dict(out=out, in_=in_, func=F.Copy), deps, G)
+
+    def mm(out, l, rh, start, stop, deps, G=None):
+        return add("t", g.tensor.matmul, dict(out=out, lhsT=l, rhs=rh, start=start, stop=stop), deps, G)
+
+    def iota(out, pat, base, cm, G=None, deps=(), small=True):
+        kw = dict(out=out, pattern=pat, base=base, channel_multiplier=cm)
+        if small:
+            kw["allow_small_or_imprecise_dtypes"] = True
+        return add("g", g.iota, kw, deps, G)
+
+    def aff(out, in_, pat, op, fillv, base, cm, deps, G=None):
+        return add("g", g.affine_select, dict(out=out, in_=in_, pattern=pat, compare_op=op, fill=fillv, base=base,
+                                              channel_multiplier=cm), deps, G)
+
+    def dma(q, out, in_, deps, G=None):
+        return add(q, g.sync.dma_start if q == "y" else act.dma_start, dict(out=out, in_=in_), deps, G, 16)
+
+    def remote(dst, out, in_, sem, mask, deps):
+        rid, pid = topo.addr(dst, core)
+        sent[0] += len(engines(mask))
+        add("g", g.remote_dma, dict(out_ap=out, in_ap=in_, remote_sem=T.sem[sem], local_sem=T.sem.sent, pid=pid,
+                                    routing_id=rid, dma_engine_mask=mask), deps)
+
+    def fused(parts, ap, deps):
+        tr = []
+        for dsts, sem, mask in parts:
+            ids = [DstId(rid=topo.addr(d, core)[0], pnc=topo.addr(d, core)[1]) for d in dsts]
+            tr.append(RemoteDMATransfer(dst_ids=ids, dma_engine_mask=mask, remote_sem=T.sem[sem], srcs=[ap], dsts=[ap] * len(ids)))
+            sent[0] += len(engines(mask))
+        add("g", g.remote_dma_fused, dict(transfers=tr, local_sem=T.sem.sent), deps)
+
+    def blk(t, a, w=128):
+        return t[:, a * w:(a + 1) * w]
+
+    if is_rank:
+        far, ftw = cores[partner[r]], twin[r]
+        eng = engines(topo.mask(core, ftw))
+        xm, sm = sum(eng[:4]), eng[4:8]
+        K, XG = grp(), [grp(), grp()]
+        dma("y", T.kraw[0:16, :], T.key[:, 0:64], (), K)
+        dma("y", T.kraw[16:32, :], T.key[:, 64:128], (), K)
+        for h in range(2):
+            dma("s", blk(T.xin, h, H), blk(T.x, h, H), (), XG[h])
+        gA, gV, gB, gC = grp(), grp(), grp(), grp()
+        iota(S("pmi", 0, 32), [[-1, 16]], 0, 1, gA)
+        iota(T.hv[0:32, :], [[16, 2], [0, 64]], 0, 0, gA)
+        for h in range(2):
+            iota(S("kcol", 64 * h, 64 * h + 64, 0, 1), [[0, 1]], 0, 1, gA)
+        for h in range(2):
+            iota(S("vcol", 64 * h, 64 * h + 64, 0, 1), [[0, 1]], h, 2, gV)
+        iota(T.km[:], [[0, 2], [1, 64]], 0, 0, gB, [gA, gV])
+        iota(T.mv[:], [[1, 2], [2, 64]], 0, 0, gB)
+        iota(T.cpat[:], [[1, 128]], 0, 0, gC)
+        iota(T.imod[:], [[0, 8], [1, 16]], 0, 0, gC)
+        iota(S("jc"), [[128, 8], [1024, 2]], 0, 1, gC)
+        for h in range(2):
+            remote(ftw, blk(T.xin, h, H), blk(T.xin, h, H), "xa", xm, [XG[h]])
+        RS, CF, hs, OH = grp(), grp(), grp(), grp()
+        for i in range(16):
+            ts(blk(T.rsl, i)[0:32, :] if False else T.rsl[0:32, i * 128:(i + 1) * 128], T.hv[0:32, :],
+               S("pmi", 0, 32, i, i + 1), A.is_equal, [gA], G=RS)
+        kcol = S("kcol", 0, 128, 0, 1)
+        ts(T.fold[:], T.km[:], kcol, A.is_equal, [gA, gB], G=CF)
+        ts(T.mb[:], T.mv[:], S("vcol", 0, 128, 0, 1), A.is_gt, [gV, gB], G=CF)
+        kb = cp(T.kb[0:32, :], T.kraw[0:32, :], [K])
+        for a in range(2):
+            for b in range(2):
+                fill(T.hself[64 * a:64 * a + 64, b:b + 1], 1.0 if a == b else 0.0, hs)
+        hsel = cp(T.hsel[:], T.hself[:], [hs])
+        kp = [grp(), grp()]
+        for i in range(16):
+            mm(blk(T.kps, i, 64), T.rsl[0:32, i * 128:(i + 1) * 128], T.kb[0:32, :], True, True, [RS, kb], kp[i // 8])
+        for i in range(16):
+            ts(T.oh[:, i::16], blk(T.kps, i, 64), kcol, A.is_equal, [gA, kp[i // 8]], G=OH)
+        sc = scan(T.sps[:], T.oh[:], [OH])
+        tot = cp(T.tot[:], T.sps[:, 1023:1024], [sc])
+        hm = mm(T.hps[0:1, 0:128], T.tot[:], T.fold[:], True, True, [tot, CF])
+        bm = mm(T.kps[:, 0:1], T.mb[:], T.tot[:], True, True, [tot, CF])
+        hr = cp(T.hrow[0:1, :], T.hps[0:1, 0:128], [hm], q="s")
+        store = dma("s", T.hland[r], T.hrow[0:1, :], [hr])
+        fused([([far, ftw], "hc", sm[0]), (near, "hd", sm[1]), (rtw, "hd", sm[2])], T.hland[r], [store])
+        pr = tt(T.prod[:], T.oh[:], T.sps[:], A.mult, [sc])
+        hb = ts(T.hb[:], T.hsel[:], T.kps[:, 0:1], A.mult, [hsel, bm])
+        tm, tci, pm = grp(), grp(), grp()
+        for q in range(8):
+            mm(blk(T.tps, q, 2), blk(T.prod, q), T.hsel[:], True, False, [pr, hsel], tm)
+            mm(blk(T.tps, q, 2), blk(T.oh, q), T.hb[:], False, True, [hb], tm)
+        ti = ts(T.ti[:], T.tps[:, 0:16], 1.0, A.subtract, [tm])
+        ts(T.tci[:, 0:16], T.ti[:], 4, A.arith_shift_right, [ti], G=tci)
+        ts(T.tci[:, 16:32], T.ti[:], 15, A.bitwise_and, [ti], G=tci)
+        tf = cp(S("tf"), T.tci[:], [tci])
+        for a in range(16):
+            if a % 4 == 0:
+                og = grp()
+            ts(blk(T.la, a), T.imod[:], S("tf", 0, 128, 16 + a, 17 + a), A.is_equal, [tf, gC], S("jc", 0, 128, a, a + 1), A.mult, og)
+            ts(blk(T.ra, a), T.cpat[:], S("tf", 0, 128, a, a + 1), A.is_equal, [tf, gC], G=og)
+            if a % 4 == 3:
+                for b in range(a - 3, a + 1):
+                    mm(T.tps[:, 0:128], blk(T.la, b), blk(T.ra, b), b == 0, b == 15, [og], pm)
+        pl = cp(T.plist[:], T.tps[:, 0:128], [pm])
+        xdeps = [pl] + XG
+    else:
+        xdeps = [("xa", 8), ("pa", 4)]
+
+    gD, gE, s0 = grp(), grp(), grp()
+    iota(T.pci[:], [[0, 1]], 0, 1, gD, small=False)
+    iota(T.q0[:], [[16, 128]], 0, 0, gD)
+    on = fill(T.ones[:], 1.0)
+    tail = fill(T.xs[:, W:W + CAP], 0.0)
+    fill(T.sx[0:12, 0:1], 0.0, s0)
+    fill(T.sx[0:12, 64:65], 0.0, s0)
+    pai = ts(T.pai[:], T.pci[:], 15, A.bitwise_and, [gD])
+    p16 = cp(S("p16", 0, 128, 0, 1), T.pai[:], [pai])
+    qi = ts(T.qi[:], T.q0[:], S("p16", 0, 128, 0, 1), A.add, [gD, p16])
+    aff(S("rcum", 0, 12, 0, 13), T.ones[0:12, 0:13], [[1, 13]], A.is_gt, 0.0, 0, -1, [on], gE)
+    iota(S("dp", 0, 64, 0, 6), [[W * (mine[1] - mine[0]), 6]], W * mine[0], 0, gE)
+
+    if is_rank:
+        remote(ftw, T.plist[:], T.plist[:], "pa", sum(sm), [pl])
+        fused([(near, "hr", sm[0])], T.hland[partner[r]], [("hc", 1)])
+        hdeps = [store, ("hc", 1), ("hd", 5), ("hr", 5)]
+    else:
+        fused([([c for c in rtw if c != core], "hr", engines(topo.mask(core, near[0]))[-1])], T.hland[r], [("hc", 1)])
+        hdeps = [("hc", 1), ("hd", 6), ("hr", 5)]
+
+    XS = grp()
+    for h in range(2):
+        cp(T.xs[:, h * H:h * H + H], T.xin[:].indirect(blk(T.plist, h, 64)), xdeps, XS, "vs"[h])
+
+    ld = dma("y", T.c2[0:12, :], T.hland[:], hdeps)
+    sx = grp()
+    for b in (0, 64):
+        scan(T.sx[0:12, b + 1:b + 64], T.c2[0:12, b:b + 63], [ld], sx)
+    rc, o13 = S("rcum", 0, 12, 0, 13), T.ones[0:12, 0:13]
+    mm(T.pps[:, 0:13], T.c2[0:12, :], rc, True, False, [ld, gE])
+    pp = mm(T.pps[:, 0:13], T.sx[0:12, :], o13, False, True, [sx, s0, on])
+    zo = ts(S("zo", 0, 64, 0, 6), S("dp", 0, 64, 0, 6), T.pps[0:64, r + 1:r + 2], A.min, [pp, gE], T.pps[0:64, r:r + 1], A.max)
+    zp = ts(S("zp", 0, 64, 0, 6), S("zo", 0, 64, 0, 6), T.pps[0:64, r:r + 1], A.subtract, [zo])
+    st = mm(T.sts[:, 0:6], T.ones[0:64, :], S("zp", 0, 64, 0, 6), True, True, [zp, on])
+
+    order = [mine[(idx + 1 + k) % 6] for k in range(6)]
+    slot = blk(T.land, r, CAP)
+    wls, self_g = [], None
+    for k, d in enumerate(order):
+        for m in range(k, k + 2 - 2 * (k % 2)):
+            e = mine.index(order[m])
+            wls.append(ts(blk(T.wl, m, 32), T.qi[:, 0:32], T.sts[:, e:e + 1], A.add, [st, qi]))
+        out = slot if d == r else blk(T.snd, k, CAP)
+        w = cp(out, T.xs[:].indirect(blk(T.wl, k, 32)), [wls[k], XS, tail], q="vs"[k % 2])
+        if d == r:
+            self_g = w
+        else:
+            remote(cores[d], slot, out, "da", send_mask(topo, core, cores[d], near[0]), [w])
+
+    if is_rank:
+        ng = fill(T.neg[:], -1.0)
+        cs = fill(S("cst"), 512.0)
+        cs2 = fill(S("cst", 0, 64, 0, 1), -512.0 * 11, deps=[cs])
+        gF, gG, dl, bq, bc, wt, dm, stores = [grp() for _ in range(8)]
+        a1, a2, a3, m1, m2 = [S(n, 0, 12) for n in ("a1", "a2", "a3", "m1", "m2")]
+        zc, zm, z = S("zc", 0, 64), S("zm", 0, 64), T.pps[0:64, 0:12]
+        aff(a1, T.ones[0:12, 0:12], [[-1, 12]], A.is_equal, 0.0, 0, 1, [on], gF)
+        aff(a2, T.ones[0:12, 0:12], [[-1, 12]], A.is_equal, 0.0, 1, 1, [on], gG)
+        aff(a3, a2, [[100, 12]], A.not_equal, 1.0, -11, 1, [gG], gF)
+        g1 = tt(m1, a1, a3, A.subtract, [gF])
+        g2 = ts(m2, a2, -1.0, A.mult, [gG])
+        Y0 = float(W * r)
+        z1 = ts(zc, z, Y0, A.max, [pp])
+        z2 = tt(zm, zc, T.pps[0:64, 1:13], A.min, [z1])
+        zz = tt(S("z", 0, 64, 1, 13), zm, z, A.subtract, [z2])
+        zw = ts(S("z", 0, 64, 0, 1), S("z", 0, 64, 12, 13), 0.0, A.add, [zz])
+        mm(T.hps[:, 0:12], T.sx[0:12, :], m1, True, False, [g1, sx, s0], dl)
+        mm(T.hps[:, 0:12], T.c2[0:12, :], m2, False, False, [g2, ld], dl)
+        mm(T.hps[:, 0:12], T.neg[0:64, :], S("z", 0, 64, 1, 13), False, False, [ng, zz], dl)
+        mm(T.hps[:, 0:12], T.ones[0:64, :], S("z", 0, 64, 0, 12), False, True, [zz, zw], dl)
+        mm(T.hps[:, 12:13], T.neg[0:64, :], S("z", 0, 64, 12, 13), True, True, [zz], dl)
+        for h in range(2):
+            p0, p1 = 64 * h, 64 * h + 64
+            ts(T.bq[p0:p1, :], T.pps[p0:p1, h:12:2], Y0, A.subtract, [pp], 0.0, A.max, bq)
+        ts(T.bci[:, 0:6], T.bq[:], 4, A.arith_shift_right, [bq], G=bc)
+        ts(T.bci[:, 6:12], T.bq[:], 15, A.bitwise_and, [bq], G=bc)
+        bf = cp(S("bf"), T.bci[:], [bc])
+        for h in range(2):
+            p0, p1 = 64 * h, 64 * h + 64
+            tt(S("wt", p0, p1, 0, 6), T.hps[p0:p1, h:12:2], S("cst", p0, p1, 0, 6), A.add, [dl, cs, cs2], wt)
+        bcol = ts(S("bcol", 0, 128, 0, 1), T.hps[:, 12:13], Y0 + 512.0 * 11, A.add, [dl])
+        for q in range(6):
+            og = grp()
+            wq, bc_, bi_ = S("wt", 0, 128, q, q + 1), S("bf", 0, 128, q, q + 1), S("bf", 0, 128, 6 + q, 7 + q)
+            ts(blk(T.r1, q), T.cpat[:], bc_, A.is_gt, [bf, wt, gC], wq, A.mult, og)
+            ts(blk(T.r2, q), T.cpat[:], bc_, A.is_equal, [bf, gC], G=og)
+            ts(blk(T.l2, q), T.imod[:], bi_, A.is_ge, [bf, wt, gC], wq, A.mult, og)
+            mm(T.kps[:, 512:640], T.ones[:], blk(T.r1, q), q == 0, False, [og, on], dm)
+            mm(T.kps[:, 512:640], blk(T.l2, q), blk(T.r2, q), False, q == 5, [og], dm)
+        of = tt(T.of[:], T.kps[:, 512:640], T.qi[:], A.add, [dm, qi])
+        yo = ts(T.yoff[:], T.of[:], S("bcol", 0, 128, 0, 1), A.add, [of, bcol])
+        nd = sum(len(engines(send_mask(topo, c, core, cores[mine[idx - 1]]))) for c in rtw + near)
+        for k in range(4):
+            w = cp(blk(T.yb, k, 512), T.land[:].indirect(blk(T.yoff, k, 32)), [yo, self_g, ("da", nd)], q="vs"[k % 2])
+            dma("y", blk(T.y, k, 512), blk(T.yb, k, 512), [w], stores)
+        add("y", None, {}, [stores])
+    add("g", None, {}, [("sent", sent[0])])
+    run(ops, {"g": g, "v": vec, "s": act, "y": g.sync, "t": g.tensor}, T)

@@ -10,14 +10,14 @@ for _n, _w in (("a1", 12), ("a2", 12), ("a3", 12), ("m1", 12), ("m2", 12), ("zc"
 SCRATCH = {"hland": ("dram", [12, 128, 1], "float32")}
 for _t, _l in (("float32", "small=%d hrow=128 q0=128 qi=128 c2=128 sx=128 ones=128 neg=128 l2=768 r1=768 r2=768 of=128"
                 % sum(w for o, w in SMALL.values())),
-               ("bfloat16", "kb=64 hv=128 km=128 mv=128 rsl=2048 hself=2 imod=128 cpat=128 xin=2048 xs=2560 snd=3072 land=6144 yb=2048"),
+               ("bfloat16", "kb=64 hv=128 km=128 mv=128 rsl=2048 hself=2 imod=128 cpat=128 xin=2048 xs=2560 xq=512 snd=3072 land=6144 yb=2048"),
                ("float16", "oh=1024 prod=1024 tot=1 fold=128 mb=128 hsel=2 hb=2 la=2048 ra=2048"),
                ("int32", "kraw=64 ti=16 tci=32 pci=1 pai=1 bq=6 bci=12"), ("uint16", "plist=128 wl=192 yoff=128")):
     for _b in _l.split():
         SCRATCH[_b.split("=")[0]] = ("sbuf", [128, int(_b.split("=")[1])], _t)
 for _b, _w in (("kps", 1024), ("sps", 1024), ("tps", 512), ("hps", 512), ("pps", 512), ("sts", 512)):
     SCRATCH[_b] = ("psum", [128, _w], "float32")
-SEMAPHORES = ["e%d" % i for i in range(NE)] + ["xa", "pa", "hd", "hc", "hr", "da", "sent"]
+SEMAPHORES = ["e%d" % i for i in range(NE)] + ["xa", "xl", "pa", "hd", "hc", "hr", "da", "sent"]
 PLANS = {}
 
 
@@ -148,27 +148,33 @@ def body(g, core, T, topo, P, r, is_rank):
         add("g", g.remote_dma, dict(out_ap=out, in_ap=in_, remote_sem=T.sem[sem], local_sem=T.sem.sent, pid=pid,
                                     routing_id=rid, dma_engine_mask=mask), deps)
 
-    def fused(parts, ap, deps):
+    def fused(parts, deps):
         tr = []
-        for dsts, sem, mask in parts:
+        for dsts, sem, mask, src, dst in parts:
             ids = [DstId(rid=topo.addr(d, core)[0], pnc=topo.addr(d, core)[1]) for d in dsts]
-            tr.append(RemoteDMATransfer(dst_ids=ids, dma_engine_mask=mask, remote_sem=T.sem[sem], srcs=[ap], dsts=[ap] * len(ids)))
+            tr.append(RemoteDMATransfer(dst_ids=ids, dma_engine_mask=mask, remote_sem=T.sem[sem], srcs=[src], dsts=[dst] * len(ids)))
             sent[0] += len(engines(mask))
         add("g", g.remote_dma_fused, dict(transfers=tr, local_sem=T.sem.sent), deps)
 
     def blk(t, a, w=128):
         return t[:, a * w:(a + 1) * w]
 
+    gA, gV, gB, gC, gD, gE, gF, gG, s0 = [grp() for _ in range(9)]
+    on = fill(T.ones[:], 1.0)
+    fill(T.sx[0:12, 0:1], 0.0, s0)
+    fill(T.sx[0:12, 64:65], 0.0, s0)
+    a1, a2, a3, m1, m2 = [S(n, 0, 12) for n in ("a1", "a2", "a3", "m1", "m2")]
+    x1 = T.xin[:, CAP:H]
+    chipm = [e for e in engines(topo.mask(core, rtw[idx] if is_rank else cores[home])) if not e & topo.mask(core, near[0])][:4]
     if is_rank:
-        far, ftw = cores[partner[r]], twin[r]
+        ftw, here = twin[r], rtw[idx]
         eng = engines(topo.mask(core, ftw))
-        xm, sm = sum(eng[:4]), eng[4:8]
+        sm, xm = eng[:4], sum(eng[4:8])
         K, XG = grp(), [grp(), grp()]
         dma("y", T.kraw[0:16, :], T.key[:, 0:64], (), K)
         dma("y", T.kraw[16:32, :], T.key[:, 64:128], (), K)
         for h in range(2):
             dma("s", blk(T.xin, h, H), blk(T.x, h, H), (), XG[h])
-        gA, gV, gB, gC = grp(), grp(), grp(), grp()
         iota(S("pmi", 0, 32), [[-1, 16]], 0, 1, gA)
         iota(T.hv[0:32, :], [[16, 2], [0, 64]], 0, 0, gA)
         for h in range(2):
@@ -180,12 +186,25 @@ def body(g, core, T, topo, P, r, is_rank):
         iota(T.cpat[:], [[1, 128]], 0, 0, gC)
         iota(T.imod[:], [[0, 8], [1, 16]], 0, 0, gC)
         iota(S("jc"), [[128, 8], [1024, 2]], 0, 1, gC)
-        for h in range(2):
-            remote(ftw, blk(T.xin, h, H), blk(T.xin, h, H), "xa", xm, [XG[h]])
+        fused([([here], "xl", sum(chipm), x1, T.xq[:]), ([ftw], "xa", xm, T.xin[:, 0:CAP], T.xin[:, 0:CAP])], [XG[0]])
+        remote(ftw, T.xin[:, H:W], T.xin[:, H:W], "xa", xm, [XG[1]])
+    iota(T.pci[:], [[0, 1]], 0, 1, gD, small=False)
+    iota(T.q0[:], [[16, 128]], 0, 0, gD)
+    aff(S("rcum", 0, 12, 0, 13), T.ones[0:12, 0:13], [[1, 13]], A.is_gt, 0.0, 0, -1, [on], gE)
+    iota(S("dp", 0, 64, 0, 6), [[W * (mine[1] - mine[0]), 6]], W * mine[0], 0, gE)
+
+    def qlist():
+        pai = ts(T.pai[:], T.pci[:], 15, A.bitwise_and, [gD])
+        p16 = ts(S("p16", 0, 128, 0, 1), T.pai[:], 0.0, A.add, [pai])
+        return ts(T.qi[:], T.q0[:], S("p16", 0, 128, 0, 1), A.add, [gD, p16])
+
+    if is_rank:
+        aff(a1, T.ones[0:12, 0:12], [[-1, 12]], A.is_equal, 0.0, 0, 1, [on], gF)
+        aff(a2, T.ones[0:12, 0:12], [[-1, 12]], A.is_equal, 0.0, 1, 1, [on], gG)
+        aff(a3, a2, [[100, 12]], A.not_equal, 1.0, -11, 1, [gG], gF)
         RS, CF, hs, OH = grp(), grp(), grp(), grp()
         for i in range(16):
-            ts(blk(T.rsl, i)[0:32, :] if False else T.rsl[0:32, i * 128:(i + 1) * 128], T.hv[0:32, :],
-               S("pmi", 0, 32, i, i + 1), A.is_equal, [gA], G=RS)
+            ts(T.rsl[0:32, i * 128:(i + 1) * 128], T.hv[0:32, :], S("pmi", 0, 32, i, i + 1), A.is_equal, [gA], G=RS)
         kcol = S("kcol", 0, 128, 0, 1)
         ts(T.fold[:], T.km[:], kcol, A.is_equal, [gA, gB], G=CF)
         ts(T.mb[:], T.mv[:], S("vcol", 0, 128, 0, 1), A.is_gt, [gV, gB], G=CF)
@@ -204,14 +223,19 @@ def body(g, core, T, topo, P, r, is_rank):
         hm = mm(T.hps[0:1, 0:128], T.tot[:], T.fold[:], True, True, [tot, CF])
         bm = mm(T.kps[:, 0:1], T.mb[:], T.tot[:], True, True, [tot, CF])
         hr = cp(T.hrow[0:1, :], T.hps[0:1, 0:128], [hm], q="s")
-        store = dma("s", T.hland[r], T.hrow[0:1, :], [hr])
-        fused([([far, ftw], "hc", sm[0]), (near, "hd", sm[1]), (rtw, "hd", sm[2])], T.hland[r], [store])
+        hl = T.hland[r]
+        store = dma("s", hl, T.hrow[0:1, :], [hr])
+        fused([([cores[partner[r]], ftw], "hc", sm[0], hl, hl), (near, "hd", sm[1], hl, hl), (rtw, "hd", sm[2], hl, hl)], [store])
+        ho = T.hland[partner[r]]
+        fused([(near, "hr", sm[0], ho, ho)], [("hc", 1)])
+        hdeps = [store, ("hc", 1), ("hd", 5), ("hr", 5)]
         pr = tt(T.prod[:], T.oh[:], T.sps[:], A.mult, [sc])
         hb = ts(T.hb[:], T.hsel[:], T.kps[:, 0:1], A.mult, [hsel, bm])
         tm, tci, pm = grp(), grp(), grp()
         for q in range(8):
             mm(blk(T.tps, q, 2), blk(T.prod, q), T.hsel[:], True, False, [pr, hsel], tm)
             mm(blk(T.tps, q, 2), blk(T.oh, q), T.hb[:], False, True, [hb], tm)
+        tail = fill(T.xs[:, W:W + CAP], 0.0)
         ti = ts(T.ti[:], T.tps[:, 0:16], 1.0, A.subtract, [tm])
         ts(T.tci[:, 0:16], T.ti[:], 4, A.arith_shift_right, [ti], G=tci)
         ts(T.tci[:, 16:32], T.ti[:], 15, A.bitwise_and, [ti], G=tci)
@@ -224,31 +248,23 @@ def body(g, core, T, topo, P, r, is_rank):
             if a % 4 == 3:
                 for b in range(a - 3, a + 1):
                     mm(T.tps[:, 0:128], blk(T.la, b), blk(T.ra, b), b == 0, b == 15, [og], pm)
+        g1 = tt(m1, a1, a3, A.subtract, [gF])
+        g2 = ts(m2, a2, -1.0, A.mult, [gG])
+        ng = fill(T.neg[:], -1.0)
+        cs = fill(S("cst"), 512.0)
+        cs2 = fill(S("cst", 0, 64, 0, 1), -512.0 * 11, deps=[cs])
         pl = cp(T.plist[:], T.tps[:, 0:128], [pm])
+        remote(ftw, T.plist[:], T.plist[:], "pa", sum(sm), [pl])
+        qi = qlist()
         xdeps = [pl] + XG
     else:
-        xdeps = [("xa", 8), ("pa", 4)]
-
-    gD, gE, s0 = grp(), grp(), grp()
-    iota(T.pci[:], [[0, 1]], 0, 1, gD, small=False)
-    iota(T.q0[:], [[16, 128]], 0, 0, gD)
-    on = fill(T.ones[:], 1.0)
-    tail = fill(T.xs[:, W:W + CAP], 0.0)
-    fill(T.sx[0:12, 0:1], 0.0, s0)
-    fill(T.sx[0:12, 64:65], 0.0, s0)
-    pai = ts(T.pai[:], T.pci[:], 15, A.bitwise_and, [gD])
-    p16 = cp(S("p16", 0, 128, 0, 1), T.pai[:], [pai])
-    qi = ts(T.qi[:], T.q0[:], S("p16", 0, 128, 0, 1), A.add, [gD, p16])
-    aff(S("rcum", 0, 12, 0, 13), T.ones[0:12, 0:13], [[1, 13]], A.is_gt, 0.0, 0, -1, [on], gE)
-    iota(S("dp", 0, 64, 0, 6), [[W * (mine[1] - mine[0]), 6]], W * mine[0], 0, gE)
-
-    if is_rank:
-        remote(ftw, T.plist[:], T.plist[:], "pa", sum(sm), [pl])
-        fused([(near, "hr", sm[0])], T.hland[partner[r]], [("hc", 1)])
-        hdeps = [store, ("hc", 1), ("hd", 5), ("hr", 5)]
-    else:
-        fused([([c for c in rtw if c != core], "hr", engines(topo.mask(core, near[0]))[-1])], T.hland[r], [("hc", 1)])
+        tail = fill(T.xs[:, W:W + CAP], 0.0)
+        eng = engines(topo.mask(core, near[0]))
+        remote(twin[home], x1, T.xq[:], "xa", sum(eng[4:8]), [("xl", len(chipm))])
+        fused([([c for c in rtw if c != core], "hr", eng[0], T.hland[r], T.hland[r])], [("hc", 1)])
         hdeps = [("hc", 1), ("hd", 6), ("hr", 5)]
+        qi = qlist()
+        xdeps = [("xa", 12), ("pa", 4)]
 
     XS = grp()
     for h in range(2):
@@ -280,17 +296,8 @@ def body(g, core, T, topo, P, r, is_rank):
             remote(cores[d], slot, out, "da", send_mask(topo, core, cores[d], near[0]), [w])
 
     if is_rank:
-        ng = fill(T.neg[:], -1.0)
-        cs = fill(S("cst"), 512.0)
-        cs2 = fill(S("cst", 0, 64, 0, 1), -512.0 * 11, deps=[cs])
-        gF, gG, dl, bq, bc, wt, dm, stores = [grp() for _ in range(8)]
-        a1, a2, a3, m1, m2 = [S(n, 0, 12) for n in ("a1", "a2", "a3", "m1", "m2")]
+        dl, bq, bc, wt, dm, stores = [grp() for _ in range(6)]
         zc, zm, z = S("zc", 0, 64), S("zm", 0, 64), T.pps[0:64, 0:12]
-        aff(a1, T.ones[0:12, 0:12], [[-1, 12]], A.is_equal, 0.0, 0, 1, [on], gF)
-        aff(a2, T.ones[0:12, 0:12], [[-1, 12]], A.is_equal, 0.0, 1, 1, [on], gG)
-        aff(a3, a2, [[100, 12]], A.not_equal, 1.0, -11, 1, [gG], gF)
-        g1 = tt(m1, a1, a3, A.subtract, [gF])
-        g2 = ts(m2, a2, -1.0, A.mult, [gG])
         Y0 = float(W * r)
         z1 = ts(zc, z, Y0, A.max, [pp])
         z2 = tt(zm, zc, T.pps[0:64, 1:13], A.min, [z1])

@@ -1,7 +1,9 @@
 from concourse.bass import DstId, RemoteDMATransfer
 from concourse.mybir import AluOpType as A, ActivationFunctionType as F
 
-N, W, CAP, H, NE = 12, 2048, 512, 1024, 95
+N, W, CAP, H, NE = 12, 2048, 512, 1024, 110
+XC = ((0, 1024), (1024, 1536), (1536, 2048))
+YC = ((0, 640), (640, 1280), (1280, 1664), (1664, 2048))
 SMALL = {}
 for _n, _w in (("a1", 12), ("a2", 12), ("a3", 12), ("m1", 12), ("m2", 12), ("zc", 12), ("zm", 12), ("cst", 8), ("wt", 8),
                ("bcol", 4), ("zo", 8), ("zp", 8), ("p16", 4), ("kcol", 4), ("vcol", 4), ("pmi", 16), ("jc", 16), ("tf", 32),
@@ -38,12 +40,6 @@ def plan(topo, cores):
 
 def engines(mask):
     return [1 << i for i in range(16) if mask >> i & 1]
-
-
-def send_mask(topo, src, dst, far):
-    m = topo.mask(src, dst)
-    off = topo.mask(src, far)
-    return m & ~off if m & ~off else m
 
 
 def grp():
@@ -164,17 +160,18 @@ def body(g, core, T, topo, P, r, is_rank):
     fill(T.sx[0:12, 0:1], 0.0, s0)
     fill(T.sx[0:12, 64:65], 0.0, s0)
     a1, a2, a3, m1, m2 = [S(n, 0, 12) for n in ("a1", "a2", "a3", "m1", "m2")]
-    x1 = T.xin[:, CAP:H]
-    chipm = [e for e in engines(topo.mask(core, rtw[idx] if is_rank else cores[home])) if not e & topo.mask(core, near[0])][:4]
+    x0, x1 = blk(T.xin, 0, 512), blk(T.xin, 1, 512)
+    eng = engines(topo.mask(core, near[0]))
+    half = len(eng) // 2
+    lo, hi = eng[:half], sum(eng[half:])
+    chipm = [e for e in engines(topo.mask(core, rtw[idx] if is_rank else cores[home])) if e not in eng][:half]
     if is_rank:
         ftw, here = twin[r], rtw[idx]
-        eng = engines(topo.mask(core, ftw))
-        sm, xm = eng[:4], sum(eng[4:8])
-        K, XG = grp(), [grp(), grp()]
+        K, XG = grp(), [grp(), grp(), grp()]
         dma("y", T.kraw[0:16, :], T.key[:, 0:64], (), K)
-        dma("y", T.kraw[16:32, :], T.key[:, 64:128], (), K)
-        for h in range(2):
-            dma("s", blk(T.xin, h, H), blk(T.x, h, H), (), XG[h])
+        dma("s", T.kraw[16:32, :], T.key[:, 64:128], (), K)
+        for h in range(3):
+            dma("s", T.xin[:, XC[h][0]:XC[h][1]], T.x[:, XC[h][0]:XC[h][1]], (), XG[h])
         iota(S("pmi", 0, 32), [[-1, 16]], 0, 1, gA)
         iota(T.hv[0:32, :], [[16, 2], [0, 64]], 0, 0, gA)
         for h in range(2):
@@ -183,15 +180,18 @@ def body(g, core, T, topo, P, r, is_rank):
             iota(S("vcol", 64 * h, 64 * h + 64, 0, 1), [[0, 1]], h, 2, gV)
         iota(T.km[:], [[0, 2], [1, 64]], 0, 0, gB, [gA, gV])
         iota(T.mv[:], [[1, 2], [2, 64]], 0, 0, gB)
+        fused([([here], "xl", sum(chipm), x1, T.xq[:]), ([ftw], "xa", hi, x0, x0)], [XG[0]])
+        xp = T.xin[:, XC[1][0]:XC[1][1]]
+        remote(ftw, xp, xp, "xa", hi, [XG[1]])
         iota(T.cpat[:], [[1, 128]], 0, 0, gC)
         iota(T.imod[:], [[0, 8], [1, 16]], 0, 0, gC)
         iota(S("jc"), [[128, 8], [1024, 2]], 0, 1, gC)
-        fused([([here], "xl", sum(chipm), x1, T.xq[:]), ([ftw], "xa", xm, T.xin[:, 0:CAP], T.xin[:, 0:CAP])], [XG[0]])
-        remote(ftw, T.xin[:, H:W], T.xin[:, H:W], "xa", xm, [XG[1]])
-    iota(T.pci[:], [[0, 1]], 0, 1, gD, small=False)
-    iota(T.q0[:], [[16, 128]], 0, 0, gD)
-    aff(S("rcum", 0, 12, 0, 13), T.ones[0:12, 0:13], [[1, 13]], A.is_gt, 0.0, 0, -1, [on], gE)
-    iota(S("dp", 0, 64, 0, 6), [[W * (mine[1] - mine[0]), 6]], W * mine[0], 0, gE)
+
+    def gconst():
+        iota(T.pci[:], [[0, 1]], 0, 1, gD, small=False)
+        iota(T.q0[:], [[16, 128]], 0, 0, gD)
+        aff(S("rcum", 0, 12, 0, 13), T.ones[0:12, 0:13], [[1, 13]], A.is_gt, 0.0, 0, -1, [on], gE)
+        iota(S("dp", 0, 64, 0, 6), [[W * (mine[1] - mine[0]), 6]], W * mine[0], 0, gE)
 
     def qlist():
         pai = ts(T.pai[:], T.pci[:], 15, A.bitwise_and, [gD])
@@ -199,20 +199,13 @@ def body(g, core, T, topo, P, r, is_rank):
         return ts(T.qi[:], T.q0[:], S("p16", 0, 128, 0, 1), A.add, [gD, p16])
 
     if is_rank:
-        aff(a1, T.ones[0:12, 0:12], [[-1, 12]], A.is_equal, 0.0, 0, 1, [on], gF)
-        aff(a2, T.ones[0:12, 0:12], [[-1, 12]], A.is_equal, 0.0, 1, 1, [on], gG)
-        aff(a3, a2, [[100, 12]], A.not_equal, 1.0, -11, 1, [gG], gF)
         RS, CF, hs, OH = grp(), grp(), grp(), grp()
         for i in range(16):
             ts(T.rsl[0:32, i * 128:(i + 1) * 128], T.hv[0:32, :], S("pmi", 0, 32, i, i + 1), A.is_equal, [gA], G=RS)
         kcol = S("kcol", 0, 128, 0, 1)
+        kb = cp(T.kb[0:32, :], T.kraw[0:32, :], [K])
         ts(T.fold[:], T.km[:], kcol, A.is_equal, [gA, gB], G=CF)
         ts(T.mb[:], T.mv[:], S("vcol", 0, 128, 0, 1), A.is_gt, [gV, gB], G=CF)
-        kb = cp(T.kb[0:32, :], T.kraw[0:32, :], [K])
-        for a in range(2):
-            for b in range(2):
-                fill(T.hself[64 * a:64 * a + 64, b:b + 1], 1.0 if a == b else 0.0, hs)
-        hsel = cp(T.hsel[:], T.hself[:], [hs])
         kp = [grp(), grp()]
         for i in range(16):
             mm(blk(T.kps, i, 64), T.rsl[0:32, i * 128:(i + 1) * 128], T.kb[0:32, :], True, True, [RS, kb], kp[i // 8])
@@ -223,13 +216,22 @@ def body(g, core, T, topo, P, r, is_rank):
         hm = mm(T.hps[0:1, 0:128], T.tot[:], T.fold[:], True, True, [tot, CF])
         bm = mm(T.kps[:, 0:1], T.mb[:], T.tot[:], True, True, [tot, CF])
         hr = cp(T.hrow[0:1, :], T.hps[0:1, 0:128], [hm], q="s")
-        hl = T.hland[r]
+        hl, ho = T.hland[r], T.hland[partner[r]]
         store = dma("s", hl, T.hrow[0:1, :], [hr])
-        fused([([cores[partner[r]], ftw], "hc", sm[0], hl, hl), (near, "hd", sm[1], hl, hl), (rtw, "hd", sm[2], hl, hl)], [store])
-        ho = T.hland[partner[r]]
-        fused([(near, "hr", sm[0], ho, ho)], [("hc", 1)])
+        fused([([cores[partner[r]], ftw], "hc", lo[0], hl, hl), (near, "hd", lo[1], hl, hl), (rtw, "hd", lo[2], hl, hl)], [store])
+        xp = T.xin[:, XC[2][0]:XC[2][1]]
+        remote(ftw, xp, xp, "xa", hi, [XG[2]])
+        gconst()
+        aff(a1, T.ones[0:12, 0:12], [[-1, 12]], A.is_equal, 0.0, 0, 1, [on], gF)
+        aff(a2, T.ones[0:12, 0:12], [[-1, 12]], A.is_equal, 0.0, 1, 1, [on], gG)
+        aff(a3, a2, [[100, 12]], A.not_equal, 1.0, -11, 1, [gG], gF)
+        fused([(near, "hr", lo[1], ho, ho), ([c for c in rtw if c != here], "hr", lo[2], ho, ho)], [("hc", 1)])
         hdeps = [store, ("hc", 1), ("hd", 5), ("hr", 5)]
         pr = tt(T.prod[:], T.oh[:], T.sps[:], A.mult, [sc])
+        for a in range(2):
+            for b in range(2):
+                fill(T.hself[64 * a:64 * a + 64, b:b + 1], 1.0 if a == b else 0.0, hs)
+        hsel = cp(T.hsel[:], T.hself[:], [hs])
         hb = ts(T.hb[:], T.hsel[:], T.kps[:, 0:1], A.mult, [hsel, bm])
         tm, tci, pm = grp(), grp(), grp()
         for q in range(8):
@@ -248,27 +250,31 @@ def body(g, core, T, topo, P, r, is_rank):
             if a % 4 == 3:
                 for b in range(a - 3, a + 1):
                     mm(T.tps[:, 0:128], blk(T.la, b), blk(T.ra, b), b == 0, b == 15, [og], pm)
-        g1 = tt(m1, a1, a3, A.subtract, [gF])
-        g2 = ts(m2, a2, -1.0, A.mult, [gG])
         ng = fill(T.neg[:], -1.0)
         cs = fill(S("cst"), 512.0)
         cs2 = fill(S("cst", 0, 64, 0, 1), -512.0 * 11, deps=[cs])
         pl = cp(T.plist[:], T.tps[:, 0:128], [pm])
-        remote(ftw, T.plist[:], T.plist[:], "pa", sum(sm), [pl])
-        qi = qlist()
+        remote(ftw, T.plist[:], T.plist[:], "pa", sum(lo), [pl])
         xdeps = [pl] + XG
     else:
         tail = fill(T.xs[:, W:W + CAP], 0.0)
-        eng = engines(topo.mask(core, near[0]))
-        remote(twin[home], x1, T.xq[:], "xa", sum(eng[4:8]), [("xl", len(chipm))])
-        fused([([c for c in rtw if c != core], "hr", eng[0], T.hland[r], T.hland[r])], [("hc", 1)])
+        gconst()
+        remote(twin[home], x1, T.xq[:], "xa", sum(eng), [("xl", len(chipm))])
         hdeps = [("hc", 1), ("hd", 6), ("hr", 5)]
         qi = qlist()
-        xdeps = [("xa", 12), ("pa", 4)]
+        xdeps = [("xa", 3 * half + len(eng)), ("pa", half)]
 
     XS = grp()
-    for h in range(2):
-        cp(T.xs[:, h * H:h * H + H], T.xin[:].indirect(blk(T.plist, h, 64)), xdeps, XS, "vs"[h])
+
+    def lsort():
+        for h in range(2):
+            cp(T.xs[:, h * H:h * H + H], T.xin[:].indirect(blk(T.plist, h, 64)), xdeps, XS, "vs"[h])
+
+    if is_rank:
+        lsort()
+        qi = qlist()
+        g1 = tt(m1, a1, a3, A.subtract, [gF])
+        g2 = ts(m2, a2, -1.0, A.mult, [gG])
 
     ld = dma("y", T.c2[0:12, :], T.hland[:], hdeps)
     sx = grp()
@@ -283,17 +289,37 @@ def body(g, core, T, topo, P, r, is_rank):
 
     order = [mine[(idx + 1 + k) % 6] for k in range(6)]
     slot = blk(T.land, r, CAP)
-    wls, self_g = [], None
-    for k, d in enumerate(order):
-        for m in range(k, k + 2 - 2 * (k % 2)):
-            e = mine.index(order[m])
-            wls.append(ts(blk(T.wl, m, 32), T.qi[:, 0:32], T.sts[:, e:e + 1], A.add, [st, qi]))
-        out = slot if d == r else blk(T.snd, k, CAP)
-        w = cp(out, T.xs[:].indirect(blk(T.wl, k, 32)), [wls[k], XS, tail], q="vs"[k % 2])
-        if d == r:
-            self_g = w
+    wls, wins = {}, [grp() for _ in range(6)]
+
+    def wlist(k):
+        e = mine.index(order[k])
+        wls[k] = ts(blk(T.wl, k, 32), T.qi[:, 0:32], T.sts[:, e:e + 1], A.add, [st, qi])
+
+    def window(k, q, a=0, b=CAP):
+        base, t = (CAP * r, T.land) if order[k] == r else (CAP * k, T.snd)
+        cp(t[:, base + a:base + b], T.xs[:].indirect(T.wl[:, 32 * k + a // 16:32 * k + b // 16]), [wls[k], XS, tail], wins[k], q)
+
+    if not is_rank:
+        for k in range(6):
+            wlist(k)
+        lsort()
+    for k, lists in ((0, (0,)), (1, (2, 1)), (3, (4, 3)), (5, (5,))):
+        if is_rank:
+            for m in lists:
+                wlist(m)
+        if k in (0, 5):
+            window(k, "v", 0, 256)
+            window(k, "s", 256, 512)
         else:
-            remote(cores[d], slot, out, "da", send_mask(topo, core, cores[d], near[0]), [w])
+            window(k, "v")
+            window(k + 1, "s")
+    remote(cores[order[0]], slot, blk(T.snd, 0, CAP), "da", sum(eng), [wins[0]])
+    p = [([cores[order[k]]], "da", sum(lo) if k % 2 else hi, blk(T.snd, k, CAP), slot) for k in range(1, 5)]
+    fused(p[:2], wins[1:3])
+    if is_rank:
+        fused(p[2:], wins[3:5])
+    else:
+        fused(p[2:] + [([cores[home]], "da", sum(chipm), blk(T.snd, 5, CAP), slot)], wins[3:6])
 
     if is_rank:
         dl, bq, bc, wt, dm, stores = [grp() for _ in range(6)]
@@ -328,10 +354,10 @@ def body(g, core, T, topo, P, r, is_rank):
             mm(T.kps[:, 512:640], blk(T.l2, q), blk(T.r2, q), False, q == 5, [og], dm)
         of = tt(T.of[:], T.kps[:, 512:640], T.qi[:], A.add, [dm, qi])
         yo = ts(T.yoff[:], T.of[:], S("bcol", 0, 128, 0, 1), A.add, [of, bcol])
-        nd = sum(len(engines(send_mask(topo, c, core, cores[mine[idx - 1]]))) for c in rtw + near)
-        for k in range(4):
-            w = cp(blk(T.yb, k, 512), T.land[:].indirect(blk(T.yoff, k, 32)), [yo, self_g, ("da", nd)], q="vs"[k % 2])
-            dma("y", blk(T.y, k, 512), blk(T.yb, k, 512), [w], stores)
+        nd = sum(len(eng) if mine[(i + 1) % 6] == home else half for i in range(6) if i != idx) * 2 + len(chipm)
+        for k, (a, b) in enumerate(YC):
+            w = cp(T.yb[:, a:b], T.land[:].indirect(T.yoff[:, a // 16:b // 16]), [yo, wins[5], ("da", nd)], q="vs"[k % 2])
+            dma("y", T.y[:, a:b], T.yb[:, a:b], [w], stores)
         add("y", None, {}, [stores])
     add("g", None, {}, [("sent", sent[0])])
     run(ops, {"g": g, "v": vec, "s": act, "y": g.sync, "t": g.tensor}, T)

@@ -2,24 +2,27 @@ from concourse.bass import DstId, RemoteDMATransfer
 from concourse.mybir import AluOpType as A, ActivationFunctionType as F
 
 N, W, CAP, H, NE = 12, 2048, 512, 1024, 110
-XC = ((0, 1024), (1024, 1536), (1536, 2048))
-YC = ((0, 640), (640, 1280), (1280, 1664), (1664, 2048))
+XP = 448
+XC = ((0, XP), (XP, 2 * XP), (2 * XP, 3 * XP), (3 * XP, W))
+YC = ((0, 256), (256, 512), (512, 896), (896, 1280), (1280, 1664), (1664, 2048))
 SMALL = {}
 for _n, _w in (("a1", 12), ("a2", 12), ("a3", 12), ("m1", 12), ("m2", 12), ("zc", 12), ("zm", 12), ("cst", 8), ("wt", 8),
-               ("bcol", 4), ("zo", 8), ("zp", 8), ("p16", 4), ("kcol", 4), ("vcol", 4), ("pmi", 16), ("jc", 16), ("tf", 32),
-               ("rcum", 16), ("dp", 8), ("z", 16), ("bf", 12)):
+               ("bcol", 4), ("zo", 8), ("zp", 8), ("p16", 4), ("kcol", 4), ("vcol", 4), ("pmi", 16), ("jc", 16), ("tf", 16),
+               ("rcum", 16), ("dp", 8), ("z", 16), ("bf", 12), ("hrow", 8), ("whi", 8), ("wlo", 8)):
     SMALL[_n] = (sum(w for o, w in SMALL.values()), _w)
 SCRATCH = {"hland": ("dram", [12, 128, 1], "float32")}
-for _t, _l in (("float32", "small=%d hrow=128 q0=128 qi=128 c2=128 sx=128 ones=128 neg=128 l2=768 r1=768 r2=768 of=128"
+for _t, _l in (("float32", "small=%d q0=128 qi=128 c2=128 sx=128 ones=128 neg=128 of=128 nul=128"
                 % sum(w for o, w in SMALL.values())),
-               ("bfloat16", "kb=64 hv=128 km=128 mv=128 rsl=2048 hself=2 imod=128 cpat=128 xin=2048 xs=2560 xq=512 snd=3072 land=6144 yb=2048"),
-               ("float16", "oh=1024 prod=1024 tot=1 fold=128 mb=128 hsel=2 hb=2 la=2048 ra=2048"),
-               ("int32", "kraw=64 ti=16 tci=32 pci=1 pai=1 bq=6 bci=12"), ("uint16", "plist=128 wl=192 yoff=128")):
+               ("bfloat16", "kb=64 hv=128 mc=256 mv=128 rsl=2048 hself=2 imod=128 cpat=128 onb=128 wh=8 l2=768 r1=768 r2=768"),
+               ("bfloat16", "xin=2048 xs=2560 snd=3072 land=6144 yb=2048"),
+               ("float16", "ha=128 hb2=128 oh=1024 prod=1024 tot=1 mb=128 hsel=2 hb=2 la=256 ra=2048 pc=128 rep=128"),
+               ("int32", "kraw=64 kq=16 khi=16 klo=16 ti=16 thi=16 tlo=16 pci=16 pai=16 bq=6 bci=12"),
+               ("uint16", "plist=128 wl=192 yoff=128 off=16")):
     for _b in _l.split():
         SCRATCH[_b.split("=")[0]] = ("sbuf", [128, int(_b.split("=")[1])], _t)
 for _b, _w in (("kps", 1024), ("sps", 1024), ("tps", 512), ("hps", 512), ("pps", 512), ("sts", 512)):
     SCRATCH[_b] = ("psum", [128, _w], "float32")
-SEMAPHORES = ["e%d" % i for i in range(NE)] + ["xa", "xl", "pa", "hd", "hc", "hr", "da", "sent"]
+SEMAPHORES = ["e%d" % i for i in range(NE)] + ["xa", "xl", "pa", "hd", "hc", "hr", "da", "yl", "sent"]
 PLANS = {}
 
 
@@ -27,13 +30,19 @@ def plan(topo, cores):
     if "p" in PLANS:
         return PLANS["p"]
     rk = [topo.rack(topo.host(c)) for c in cores]
-    p = {"partner": [], "twin": [], "rack": [[q for q in range(N) if rk[q] == rk[r]] for r in range(N)]}
+    p = {"partner": [], "twin": [], "help": [], "list": [],
+         "rack": [[q for q in range(N) if rk[q] == rk[r]] for r in range(N)]}
+    on_chip = [[k for k in range(512) if topo.host(k) == topo.host(c) and topo.chip(k) == topo.chip(c)] for c in cores]
     for r, c in enumerate(cores):
         s = [q for q in range(N) if rk[q] != rk[r] and topo.chip(cores[q]) == topo.chip(c) and topo.may_write(c, cores[q])][0]
-        d = cores[s]
         p["partner"].append(s)
-        p["twin"].append([k for k in range(512) if topo.host(k) == topo.host(d) and topo.chip(k) == topo.chip(d) and
-                          topo.die(k) != topo.die(d) and all(topo.may_write(k, cores[q]) for q in p["rack"][s])][0])
+        p["twin"].append([k for k in on_chip[s] if topo.die(k) != topo.die(cores[s]) and
+                          all(topo.may_write(k, cores[q]) for q in p["rack"][s])][0])
+    for r, c in enumerate(cores):
+        pairs = zip(on_chip[r][::2], on_chip[r][1::2])
+        h = [[k for k in two if k not in p["twin"] and topo.may_write(k, p["twin"][r])][-1] for two in pairs if c not in two]
+        p["help"].append(h)
+        p["list"].append([k for k in on_chip[r] if topo.die(k) == topo.die(c) and k != c and k not in h][0])
     PLANS["p"] = p
     return p
 
@@ -74,17 +83,23 @@ def rank_program(g, core, T, topo):
     P = plan(topo, T.cores)
     r = T.rank_of(core)
     if r is not None:
-        body(g, core, T, topo, P, r, True)
+        body(g, core, T, topo, P, r, "rank")
     elif core in P["twin"]:
-        body(g, core, T, topo, P, P["twin"].index(core), False)
+        body(g, core, T, topo, P, P["twin"].index(core), "twin")
+    else:
+        for r in range(N):
+            if core in P["help"][r] or core == P["list"][r]:
+                body(g, core, T, topo, P, r, "list" if core == P["list"][r] else "help")
 
 
-def body(g, core, T, topo, P, r, is_rank):
-    cores, partner, twin = T.cores, P["partner"], P["twin"]
+def body(g, core, T, topo, P, r, role):
+    cores, partner, twin, lists_ = T.cores, P["partner"], P["twin"], P["list"]
+    is_rank, is_list = role == "rank", role == "list"
     vec, act = g.vector, g.scalar
-    home = r if is_rank else partner[r]
+    home = partner[r] if role == "twin" else r
     mine = P["rack"][home]
     rtw = [twin[partner[s]] for s in mine]
+    rli = [lists_[s] for s in mine]
     idx = mine.index(home)
     near = [cores[s] for s in mine if s != home]
     ops, sent = [], [0]
@@ -111,8 +126,8 @@ def body(g, core, T, topo, P, r, is_rank):
     def tt(out, a, b, op, deps, G=None):
         return add("v", vec.tensor_tensor, dict(out=out, in0=a, in1=b, op=op), deps, G)
 
-    def scan(out, d, deps, G=None):
-        return add("v", vec.tensor_tensor_scan, dict(out=out, data0=d, data1=d, initial=0.0, op0=A.add, op1=A.max), deps, G)
+    def scan(out, d, deps, G=None, first=0.0):
+        return add("v", vec.tensor_tensor_scan, dict(out=out, data0=d, data1=d, initial=first, op0=A.add, op1=A.max), deps, G)
 
     def fill(ap, c, G=None, deps=()):
         return add("v", vec.memset, dict(ap=ap, constant=c), deps, G)
@@ -155,126 +170,177 @@ def body(g, core, T, topo, P, r, is_rank):
     def blk(t, a, w=128):
         return t[:, a * w:(a + 1) * w]
 
-    gA, gV, gB, gC, gD, gE, gF, gG, s0 = [grp() for _ in range(9)]
-    on = fill(T.ones[:], 1.0)
-    fill(T.sx[0:12, 0:1], 0.0, s0)
-    fill(T.sx[0:12, 64:65], 0.0, s0)
-    a1, a2, a3, m1, m2 = [S(n, 0, 12) for n in ("a1", "a2", "a3", "m1", "m2")]
-    x0, x1 = blk(T.xin, 0, 512), blk(T.xin, 1, 512)
-    eng = engines(topo.mask(core, near[0]))
+    def finish():
+        add("g", None, {}, [("sent", sent[0])])
+        run(ops, {"g": g, "v": vec, "s": act, "y": g.sync, "t": g.tensor}, T)
+
+    eng = engines(topo.mask(cores[r] if is_list else core, twin[r] if role == "help" else near[0]))
     half = len(eng) // 2
     lo, hi = eng[:half], sum(eng[half:])
-    chipm = [e for e in engines(topo.mask(core, rtw[idx] if is_rank else cores[home])) if e not in eng][:half]
-    if is_rank:
-        ftw, here = twin[r], rtw[idx]
-        K, XG = grp(), [grp(), grp(), grp()]
-        dma("y", T.kraw[0:16, :], T.key[:, 0:64], (), K)
-        dma("s", T.kraw[16:32, :], T.key[:, 64:128], (), K)
-        for h in range(3):
-            dma("s", T.xin[:, XC[h][0]:XC[h][1]], T.x[:, XC[h][0]:XC[h][1]], (), XG[h])
-        iota(S("pmi", 0, 32), [[-1, 16]], 0, 1, gA)
-        iota(T.hv[0:32, :], [[16, 2], [0, 64]], 0, 0, gA)
-        for h in range(2):
-            iota(S("kcol", 64 * h, 64 * h + 64, 0, 1), [[0, 1]], 0, 1, gA)
-        for h in range(2):
-            iota(S("vcol", 64 * h, 64 * h + 64, 0, 1), [[0, 1]], h, 2, gV)
-        iota(T.km[:], [[0, 2], [1, 64]], 0, 0, gB, [gA, gV])
-        iota(T.mv[:], [[1, 2], [2, 64]], 0, 0, gB)
-        fused([([here], "xl", sum(chipm), x1, T.xq[:]), ([ftw], "xa", hi, x0, x0)], [XG[0]])
-        xp = T.xin[:, XC[1][0]:XC[1][1]]
-        remote(ftw, xp, xp, "xa", hi, [XG[1]])
+    chipm = [e for e in engines(topo.mask(core, cores[home] if not is_rank else rtw[idx])) if e not in eng][:2 * half]
+
+    if role == "help":
+        part = blk(T.xin, P["help"][r].index(core), XP)
+        remote(twin[r], part, part, "xa", sum(eng), [("xl", len(chipm))])
+        finish()
+        return
+
+    gA, gH, gK, gM, gV, gC, gD, gE, gF, gG, gP, s0 = [grp() for _ in range(12)]
+    a1, a2, a3, m1, m2 = [S(n, 0, 12) for n in ("a1", "a2", "a3", "m1", "m2")]
+
+    def pats():
         iota(T.cpat[:], [[1, 128]], 0, 0, gC)
         iota(T.imod[:], [[0, 8], [1, 16]], 0, 0, gC)
-        iota(S("jc"), [[128, 8], [1024, 2]], 0, 1, gC)
 
-    def gconst():
-        iota(T.pci[:], [[0, 1]], 0, 1, gD, small=False)
+    def gconst(on):
         iota(T.q0[:], [[16, 128]], 0, 0, gD)
         aff(S("rcum", 0, 12, 0, 13), T.ones[0:12, 0:13], [[1, 13]], A.is_gt, 0.0, 0, -1, [on], gE)
         iota(S("dp", 0, 64, 0, 6), [[W * (mine[1] - mine[0]), 6]], W * mine[0], 0, gE)
 
-    def qlist():
-        pai = ts(T.pai[:], T.pci[:], 15, A.bitwise_and, [gD])
-        p16 = ts(S("p16", 0, 128, 0, 1), T.pai[:], 0.0, A.add, [pai])
+    def pmod():
+        return ts(T.pai[:], T.pci[:], 15, A.bitwise_and, [gP])
+
+    def qlist(pai):
+        p16 = ts(S("p16", 0, 128, 0, 1), T.pai[:, 0:1], 0.0, A.add, [pai])
         return ts(T.qi[:], T.q0[:], S("p16", 0, 128, 0, 1), A.add, [gD, p16])
 
+    def zeros():
+        fill(T.sx[0:12, 0:1], 0.0, s0)
+        fill(T.sx[0:12, 64:65], 0.0, s0)
+
     if is_rank:
-        RS, CF, hs, OH = grp(), grp(), grp(), grp()
+        ftw, here = twin[r], rtw[idx]
+        K, KQ, XG, RS = grp(), grp(), [grp() for _ in XC], grp()
+        dma("y", T.kraw[0:16, :], T.key[:, 0:64], (), K)
+        dma("s", T.kraw[16:32, :], T.key[:, 64:128], (), K)
+        dma("y", T.kq[:], T.key[:], (), KQ)
+        for h in range(4):
+            dma("s", T.xin[:, XC[h][0]:XC[h][1]], T.x[:, XC[h][0]:XC[h][1]], (), XG[h])
+        iota(S("pmi", 0, 32), [[-1, 16]], 0, 1, gA)
+        for h in range(2):
+            p0, p1 = 64 * h, 64 * h + 64
+            iota(S("kcol", p0, p1, 0, 1), [[0, 1]], 0, 1, gK)
+            iota(T.hself[p0:p1, :], [[2 * h - 1, 2]], 1 - h, 0, gV)
+            iota(S("vcol", p0, p1, 0, 1), [[0, 1]], h, 2, gV)
+        iota(T.pci[:], [[0, 16]], 0, 1, gP, [gK, gV], small=False)
+        iota(T.mc[:], [[1, 16], [0, 16]], 0, 0, gM)
+        iota(T.mv[:], [[1, 2], [2, 64]], 0, 0, gM)
+        for h in range(2):
+            fill(T.hv[0:32, 64 * h:64 * h + 64], 16.0 * h, gH)
         for i in range(16):
-            ts(T.rsl[0:32, i * 128:(i + 1) * 128], T.hv[0:32, :], S("pmi", 0, 32, i, i + 1), A.is_equal, [gA], G=RS)
+            ts(T.rsl[0:32, i * 128:(i + 1) * 128], T.hv[0:32, :], S("pmi", 0, 32, i, i + 1), A.is_equal, [gA, gH], G=RS)
+        pai = pmod()
+        off = cp(T.off[:], T.pai[:], [pai])
+        for k, c in enumerate(P["help"][r]):
+            remote(c, blk(T.xin, k, XP), blk(T.xin, k, XP), "xl", sum(chipm), [XG[k]])
+        pats()
+        iota(S("jc"), [[128, 8], [1024, 2]], 0, 1, gC)
+
         kcol = S("kcol", 0, 128, 0, 1)
         kb = cp(T.kb[0:32, :], T.kraw[0:32, :], [K])
-        ts(T.fold[:], T.km[:], kcol, A.is_equal, [gA, gB], G=CF)
-        ts(T.mb[:], T.mv[:], S("vcol", 0, 128, 0, 1), A.is_gt, [gV, gB], G=CF)
+        hk = ts(T.khi[:], T.kq[:], 3, A.arith_shift_right, [KQ])
+        lk = ts(T.klo[:], T.kq[:], 7, A.bitwise_and, [KQ])
+        ha = tt(T.ha[:], T.khi[:].indirect(T.off[:, 0:8]), T.mc[:, 0:128], A.is_equal, [hk, off, gM])
+        hb2 = tt(T.hb2[:], T.klo[:].indirect(T.off[:, 0:8]), T.mc[:, 0:128], A.is_equal, [lk, off, gM])
         kp = [grp(), grp()]
-        for i in range(16):
-            mm(blk(T.kps, i, 64), T.rsl[0:32, i * 128:(i + 1) * 128], T.kb[0:32, :], True, True, [RS, kb], kp[i // 8])
-        for i in range(16):
-            ts(T.oh[:, i::16], blk(T.kps, i, 64), kcol, A.is_equal, [gA, kp[i // 8]], G=OH)
-        sc = scan(T.sps[:], T.oh[:], [OH])
-        tot = cp(T.tot[:], T.sps[:, 1023:1024], [sc])
-        hm = mm(T.hps[0:1, 0:128], T.tot[:], T.fold[:], True, True, [tot, CF])
-        bm = mm(T.kps[:, 0:1], T.mb[:], T.tot[:], True, True, [tot, CF])
-        hr = cp(T.hrow[0:1, :], T.hps[0:1, 0:128], [hm], q="s")
+
+        def spread(b):
+            for i in range(16):
+                mm(T.kps[:, 512 * b + i:512 * b + 512:16], T.rsl[0:32, i * 128:(i + 1) * 128], T.kb[0:32, 32 * b:32 * b + 32],
+                   True, True, [RS, kb], kp[b])
+
+        spread(0)
+        hm = grp()
+        for q in range(16):
+            mm(T.hps[0:8, 0:8], T.ha[:, q:128:16], T.hb2[:, q:128:16], q == 0, q == 15, [ha, hb2], hm)
+        spread(1)
+        hr = cp(S("hrow", 0, 8), T.hps[0:8, 0:8], [hm], q="s")
+        store = grp()
+        for h in range(2):
+            dma("ys"[h], T.hland[r, 64 * h:64 * h + 64, :], S("hrow", 0, 8), [hr], store)
         hl, ho = T.hland[r], T.hland[partner[r]]
-        store = dma("s", hl, T.hrow[0:1, :], [hr])
-        fused([([cores[partner[r]], ftw], "hc", lo[0], hl, hl), (near, "hd", lo[1], hl, hl), (rtw, "hd", lo[2], hl, hl)], [store])
-        xp = T.xin[:, XC[2][0]:XC[2][1]]
-        remote(ftw, xp, xp, "xa", hi, [XG[2]])
-        gconst()
-        aff(a1, T.ones[0:12, 0:12], [[-1, 12]], A.is_equal, 0.0, 0, 1, [on], gF)
-        aff(a2, T.ones[0:12, 0:12], [[-1, 12]], A.is_equal, 0.0, 1, 1, [on], gG)
-        aff(a3, a2, [[100, 12]], A.not_equal, 1.0, -11, 1, [gG], gF)
-        fused([(near, "hr", lo[1], ho, ho), ([c for c in rtw if c != here], "hr", lo[2], ho, ho)], [("hc", 1)])
+        fused([([cores[partner[r]], ftw], "hc", lo[0], hl, hl), (near, "hd", lo[1], hl, hl), (rtw, "hd", lo[2], hl, hl),
+               (rli, "hd", lo[3], hl, hl)], [store])
+        xp = T.xin[:, XC[3][0]:XC[3][1]]
+        remote(ftw, xp, xp, "xa", hi, [XG[3]])
+        on = fill(T.ones[:], 1.0)
+        hsel = cp(T.hsel[:], T.hself[:], [gV])
+        mb = ts(T.mb[:], T.mv[:], S("vcol", 0, 128, 0, 1), A.is_gt, [gV, gM])
+        gconst(on)
+        oh, sc = [grp(), grp()], [grp(), grp()]
+        for b in range(2):
+            c0, c1 = 512 * b, 512 * b + 512
+            ts(T.oh[:, c0:c1], T.kps[:, c0:c1], kcol, A.is_equal, [gK, kp[b]], G=oh[b])
+            scan(T.sps[:, c0:c1], T.oh[:, c0:c1], [oh[b]] + sc[:b], sc[b], T.sps[:, c0 - 1:c0] if b else 0.0)
+        fused([(near, "hr", lo[1], ho, ho), ([c for c in rtw if c != here], "hr", lo[2], ho, ho), (rli, "hr", lo[3], ho, ho)],
+              [("hc", 1)])
         hdeps = [store, ("hc", 1), ("hd", 5), ("hr", 5)]
-        pr = tt(T.prod[:], T.oh[:], T.sps[:], A.mult, [sc])
-        for a in range(2):
-            for b in range(2):
-                fill(T.hself[64 * a:64 * a + 64, b:b + 1], 1.0 if a == b else 0.0, hs)
-        hsel = cp(T.hsel[:], T.hself[:], [hs])
-        hb = ts(T.hb[:], T.hsel[:], T.kps[:, 0:1], A.mult, [hsel, bm])
-        tm, tci, pm = grp(), grp(), grp()
-        for q in range(8):
-            mm(blk(T.tps, q, 2), blk(T.prod, q), T.hsel[:], True, False, [pr, hsel], tm)
-            mm(blk(T.tps, q, 2), blk(T.oh, q), T.hb[:], False, True, [hb], tm)
+        tot = cp(T.tot[:], T.sps[:, 1023:1024], [sc[1]])
+        bm = mm(T.sts[:, 0:1], T.mb[:], T.tot[:], True, True, [tot, mb])
+        tm = grp()
+        for c in range(4):
+            cols = slice(256 * c, 256 * c + 256)
+            pr = tt(T.prod[:, cols], T.oh[:, cols], T.sps[:, cols], A.mult, sc)
+            if c == 0:
+                hb = ts(T.hb[:], T.hsel[:], T.sts[:, 0:1], A.mult, [hsel, bm])
+            for q in (2 * c, 2 * c + 1):
+                mm(blk(T.tps, q, 2), blk(T.prod, q), T.hsel[:], True, False, [pr, hsel], tm)
+                mm(blk(T.tps, q, 2), blk(T.oh, q), T.hb[:], False, True, [hb], tm)
+        rep = ts(T.rep[0:16, :], T.imod[0:16, :], S("kcol", 0, 16, 0, 1), A.is_equal, [gC, gK])
         tail = fill(T.xs[:, W:W + CAP], 0.0)
         ti = ts(T.ti[:], T.tps[:, 0:16], 1.0, A.subtract, [tm])
-        ts(T.tci[:, 0:16], T.ti[:], 4, A.arith_shift_right, [ti], G=tci)
-        ts(T.tci[:, 16:32], T.ti[:], 15, A.bitwise_and, [ti], G=tci)
-        tf = cp(S("tf"), T.tci[:], [tci])
+        th = ts(T.thi[:], T.ti[:], 4, A.arith_shift_right, [ti])
+        tl = ts(T.tlo[:], T.ti[:], 15, A.bitwise_and, [ti])
+        tf = cp(S("tf"), T.thi[:], [th])
+        la = tt(T.la[:], T.tlo[:].indirect(T.off[:]), T.mc[:], A.is_equal, [tl, off, gM])
+        pm = grp()
         for a in range(16):
-            if a % 4 == 0:
+            if a % 2 == 0:
                 og = grp()
-            ts(blk(T.la, a), T.imod[:], S("tf", 0, 128, 16 + a, 17 + a), A.is_equal, [tf, gC], S("jc", 0, 128, a, a + 1), A.mult, og)
-            ts(blk(T.ra, a), T.cpat[:], S("tf", 0, 128, a, a + 1), A.is_equal, [tf, gC], G=og)
-            if a % 4 == 3:
-                for b in range(a - 3, a + 1):
-                    mm(T.tps[:, 0:128], blk(T.la, b), blk(T.ra, b), b == 0, b == 15, [og], pm)
-        ng = fill(T.neg[:], -1.0)
-        cs = fill(S("cst"), 512.0)
-        cs2 = fill(S("cst", 0, 64, 0, 1), -512.0 * 11, deps=[cs])
-        pl = cp(T.plist[:], T.tps[:, 0:128], [pm])
+            ts(blk(T.ra, a), T.cpat[:], S("tf", 0, 128, a, a + 1), A.is_equal, [tf, gC], S("jc", 0, 128, a, a + 1), A.mult, og)
+            if a % 2 == 1:
+                for b in (a - 1, a):
+                    mm(T.tps[0:16, 0:128], T.la[:, b:256:16], blk(T.ra, b), b == 0, b == 15, [la, og], pm)
+        pc = cp(T.pc[0:16, :], T.tps[0:16, 0:128], [pm])
+        pr = mm(T.sps[:, 0:128], T.rep[0:16, :], T.pc[0:16, :], True, True, [pc, rep])
+        pl = cp(T.plist[:], T.sps[:, 0:128], [pr])
         remote(ftw, T.plist[:], T.plist[:], "pa", sum(lo), [pl])
         xdeps = [pl] + XG
     else:
-        tail = fill(T.xs[:, W:W + CAP], 0.0)
-        gconst()
-        remote(twin[home], x1, T.xq[:], "xa", sum(eng), [("xl", len(chipm))])
-        hdeps = [("hc", 1), ("hd", 6), ("hr", 5)]
-        qi = qlist()
-        xdeps = [("xa", 3 * half + len(eng)), ("pa", half)]
+        on = fill(T.ones[:], 1.0)
+        zeros()
+        iota(T.pci[:], [[0, 16]], 0, 1, gP, small=False)
+        gconst(on)
+        pai = pmod()
+        qi = qlist(pai)
+        if is_list:
+            pats()
+            aff(a1, T.ones[0:12, 0:12], [[-1, 12]], A.is_equal, 0.0, 0, 1, [on], gF)
+            aff(a2, T.ones[0:12, 0:12], [[-1, 12]], A.is_equal, 0.0, 1, 1, [on], gG)
+            aff(a3, a2, [[100, 12]], A.not_equal, 1.0, -11, 1, [gG], gF)
+            g1 = tt(m1, a1, a3, A.subtract, [gF])
+            g2 = ts(m2, a2, -1.0, A.mult, [gG])
+            ng = fill(T.neg[:], -1.0)
+            cs = fill(S("cst"), 512.0)
+            cs2 = fill(S("cst", 0, 64, 0, 1), -512.0 * 11, deps=[cs])
+            onb, nul = fill(T.onb[:], 1.0), grp()
+            fill(T.of[:], 0.0, nul)
+            fill(T.nul[:], 0.0, nul)
+            hdeps = [("hd", 6), ("hr", 6)]
+        else:
+            tail = fill(T.xs[:, W:W + CAP], 0.0)
+            hdeps = [("hc", 1), ("hd", 6), ("hr", 5)]
+            xdeps = [("xa", 3 * len(eng) + half), ("pa", half)]
 
     XS = grp()
 
-    def lsort():
-        for h in range(2):
-            cp(T.xs[:, h * H:h * H + H], T.xin[:].indirect(blk(T.plist, h, 64)), xdeps, XS, "vs"[h])
+    def lsort(pieces):
+        for q, a, b in pieces:
+            cp(T.xs[:, a:b], T.xin[:].indirect(T.plist[:, a // 16:b // 16]), xdeps, XS, q)
 
     if is_rank:
-        lsort()
-        qi = qlist()
-        g1 = tt(m1, a1, a3, A.subtract, [gF])
-        g2 = ts(m2, a2, -1.0, A.mult, [gG])
+        lsort((("s", H, W), ("v", 0, 512)))
+        zeros()
 
     ld = dma("y", T.c2[0:12, :], T.hland[:], hdeps)
     sx = grp()
@@ -283,46 +349,52 @@ def body(g, core, T, topo, P, r, is_rank):
     rc, o13 = S("rcum", 0, 12, 0, 13), T.ones[0:12, 0:13]
     mm(T.pps[:, 0:13], T.c2[0:12, :], rc, True, False, [ld, gE])
     pp = mm(T.pps[:, 0:13], T.sx[0:12, :], o13, False, True, [sx, s0, on])
-    zo = ts(S("zo", 0, 64, 0, 6), S("dp", 0, 64, 0, 6), T.pps[0:64, r + 1:r + 2], A.min, [pp, gE], T.pps[0:64, r:r + 1], A.max)
-    zp = ts(S("zp", 0, 64, 0, 6), S("zo", 0, 64, 0, 6), T.pps[0:64, r:r + 1], A.subtract, [zo])
-    st = mm(T.sts[:, 0:6], T.ones[0:64, :], S("zp", 0, 64, 0, 6), True, True, [zp, on])
 
-    order = [mine[(idx + 1 + k) % 6] for k in range(6)]
-    slot = blk(T.land, r, CAP)
-    wls, wins = {}, [grp() for _ in range(6)]
-
-    def wlist(k):
-        e = mine.index(order[k])
-        wls[k] = ts(blk(T.wl, k, 32), T.qi[:, 0:32], T.sts[:, e:e + 1], A.add, [st, qi])
-
-    def window(k, q, a=0, b=CAP):
-        base, t = (CAP * r, T.land) if order[k] == r else (CAP * k, T.snd)
-        cp(t[:, base + a:base + b], T.xs[:].indirect(T.wl[:, 32 * k + a // 16:32 * k + b // 16]), [wls[k], XS, tail], wins[k], q)
-
-    if not is_rank:
-        for k in range(6):
-            wlist(k)
-        lsort()
-    for k, lists in ((0, (0,)), (1, (2, 1)), (3, (4, 3)), (5, (5,))):
+    if not is_list:
         if is_rank:
-            for m in lists:
-                wlist(m)
-        if k in (0, 5):
-            window(k, "v", 0, 256)
-            window(k, "s", 256, 512)
-        else:
-            window(k, "v")
-            window(k + 1, "s")
-    remote(cores[order[0]], slot, blk(T.snd, 0, CAP), "da", sum(eng), [wins[0]])
-    p = [([cores[order[k]]], "da", sum(lo) if k % 2 else hi, blk(T.snd, k, CAP), slot) for k in range(1, 5)]
-    fused(p[:2], wins[1:3])
-    if is_rank:
-        fused(p[2:], wins[3:5])
-    else:
-        fused(p[2:] + [([cores[home]], "da", sum(chipm), blk(T.snd, 5, CAP), slot)], wins[3:6])
+            lsort((("v", 512, 768),))
+            qi = qlist(pai)
+        zo = ts(S("zo", 0, 64, 0, 6), S("dp", 0, 64, 0, 6), T.pps[0:64, r + 1:r + 2], A.min, [pp, gE], T.pps[0:64, r:r + 1], A.max)
+        zp = ts(S("zp", 0, 64, 0, 6), S("zo", 0, 64, 0, 6), T.pps[0:64, r:r + 1], A.subtract, [zo])
+        st = mm(T.sts[:, 0:6], T.ones[0:64, :], S("zp", 0, 64, 0, 6), True, True, [zp, on])
+        if is_rank:
+            lsort((("v", 768, H),))
 
-    if is_rank:
-        dl, bq, bc, wt, dm, stores = [grp() for _ in range(6)]
+        order = [mine[(idx + 1 + k) % 6] for k in range(6)]
+        slot = blk(T.land, r, CAP)
+        wls, wins = {}, [grp() for _ in range(6)]
+
+        def wlist(k):
+            e = mine.index(order[k])
+            wls[k] = ts(blk(T.wl, k, 32), T.qi[:, 0:32], T.sts[:, e:e + 1], A.add, [st, qi])
+
+        def window(k, q, a=0, b=CAP):
+            base, t = (CAP * r, T.land) if order[k] == r else (CAP * k, T.snd)
+            cp(t[:, base + a:base + b], T.xs[:].indirect(T.wl[:, 32 * k + a // 16:32 * k + b // 16]), [wls[k], XS, tail], wins[k], q)
+
+        if not is_rank:
+            for k in range(6):
+                wlist(k)
+            lsort((("v", 0, H), ("s", H, W)))
+        for k, lists in ((0, (0,)), (1, (2, 1)), (3, (4, 3)), (5, (5,))):
+            if is_rank:
+                for m in lists:
+                    wlist(m)
+            if k in (0, 5):
+                window(k, "v", 0, 256)
+                window(k, "s", 256, 512)
+            else:
+                window(k, "v")
+                window(k + 1, "s")
+        remote(cores[order[0]], slot, blk(T.snd, 0, CAP), "da", sum(eng), [wins[0]])
+        p = [([cores[order[k]]], "da", sum(lo) if k % 2 else hi, blk(T.snd, k, CAP), slot) for k in range(1, 5)]
+        fused(p[:2], wins[1:3])
+        if is_rank:
+            fused(p[2:], wins[3:5])
+        else:
+            fused(p[2:] + [([cores[home]], "da", sum(chipm[:half]), blk(T.snd, 5, CAP), slot)], wins[3:6])
+    else:
+        dl, bq, bc, wt, dm = [grp() for _ in range(5)]
         zc, zm, z = S("zc", 0, 64), S("zm", 0, 64), T.pps[0:64, 0:12]
         Y0 = float(W * r)
         z1 = ts(zc, z, Y0, A.max, [pp])
@@ -344,20 +416,31 @@ def body(g, core, T, topo, P, r, is_rank):
             p0, p1 = 64 * h, 64 * h + 64
             tt(S("wt", p0, p1, 0, 6), T.hps[p0:p1, h:12:2], S("cst", p0, p1, 0, 6), A.add, [dl, cs, cs2], wt)
         bcol = ts(S("bcol", 0, 128, 0, 1), T.hps[:, 12:13], Y0 + 512.0 * 11, A.add, [dl])
+        wr = cp(T.wh[:, 0:6], S("wt", 0, 128, 0, 6), [wt])
+        wh = cp(S("whi", 0, 128, 0, 6), T.wh[:, 0:6], [wr])
+        wl = tt(S("wlo", 0, 128, 0, 6), S("wt", 0, 128, 0, 6), T.wh[:, 0:6], A.subtract, [wt, wr])
         for q in range(6):
             og = grp()
-            wq, bc_, bi_ = S("wt", 0, 128, q, q + 1), S("bf", 0, 128, q, q + 1), S("bf", 0, 128, 6 + q, 7 + q)
-            ts(blk(T.r1, q), T.cpat[:], bc_, A.is_gt, [bf, wt, gC], wq, A.mult, og)
-            ts(blk(T.r2, q), T.cpat[:], bc_, A.is_equal, [bf, gC], G=og)
-            ts(blk(T.l2, q), T.imod[:], bi_, A.is_ge, [bf, wt, gC], wq, A.mult, og)
-            mm(T.kps[:, 512:640], T.ones[:], blk(T.r1, q), q == 0, False, [og, on], dm)
-            mm(T.kps[:, 512:640], blk(T.l2, q), blk(T.r2, q), False, q == 5, [og], dm)
-        of = tt(T.of[:], T.kps[:, 512:640], T.qi[:], A.add, [dm, qi])
-        yo = ts(T.yoff[:], T.of[:], S("bcol", 0, 128, 0, 1), A.add, [of, bcol])
-        nd = sum(len(eng) if mine[(i + 1) % 6] == home else half for i in range(6) if i != idx) * 2 + len(chipm)
+            bc_, bi_ = S("bf", 0, 128, q, q + 1), S("bf", 0, 128, 6 + q, 7 + q)
+            ts(blk(T.l2, q), T.imod[:], bi_, A.is_ge, [bf, gC], G=og)
+            ts(blk(T.r1, q), T.cpat[:], bc_, A.is_equal, [bf, wh, gC], S("whi", 0, 128, q, q + 1), A.mult, og)
+            ts(blk(T.r2, q), T.cpat[:], bc_, A.is_equal, [bf, wl, gC], S("wlo", 0, 128, q, q + 1), A.mult, og)
+            for k, rr in enumerate((T.r1, T.r2)):
+                first, last = (q, k) == (0, 0), (q, k) == (5, 1)
+                mm(T.kps[:, 512:640], T.onb[:], blk(rr, q), first, last, [og, onb], dm)
+                mm(T.sps[:, 512:640], blk(T.l2, q), blk(rr, q), first, last, [og], dm)
+        of = add("v", vec.tensor_tensor_scan, dict(out=T.of[:, 1:128], data0=T.kps[:, 512:639], data1=T.nul[:, 0:127],
+                                                   initial=0.0, op0=A.add, op1=A.add), [dm, nul])
+        of2 = tt(T.of[:], T.of[:], T.sps[:, 512:640], A.add, [of])
+        of3 = tt(T.of[:], T.of[:], T.qi[:], A.add, [of2, qi])
+        yo = ts(T.yoff[:], T.of[:], S("bcol", 0, 128, 0, 1), A.add, [of3, bcol])
+        remote(cores[r], T.yoff[:], T.yoff[:], "yl", sum(chipm[:half]), [yo])
+
+    if is_rank:
+        stores = grp()
+        nd = sum(len(eng) if mine[(i + 1) % 6] == home else half for i in range(6) if i != idx) * 2 + half
         for k, (a, b) in enumerate(YC):
-            w = cp(T.yb[:, a:b], T.land[:].indirect(T.yoff[:, a // 16:b // 16]), [yo, wins[5], ("da", nd)], q="vs"[k % 2])
+            w = cp(T.yb[:, a:b], T.land[:].indirect(T.yoff[:, a // 16:b // 16]), [wins[5], ("yl", half), ("da", nd)], q="vs"[k % 2])
             dma("y", T.y[:, a:b], T.yb[:, a:b], [w], stores)
         add("y", None, {}, [stores])
-    add("g", None, {}, [("sent", sent[0])])
-    run(ops, {"g": g, "v": vec, "s": act, "y": g.sync, "t": g.tensor}, T)
+    finish()

from concourse.bass import DstId, RemoteDMATransfer
from concourse.mybir import AluOpType as A, ActivationFunctionType as F

N, W, CAP, H, NE = 12, 2048, 512, 1024, 110
XP = 448
XC = ((0, XP), (XP, 2 * XP), (2 * XP, 3 * XP), (3 * XP, W))
YC = ((0, 256), (256, 512), (512, 896), (896, 1280), (1280, 1664), (1664, 2048))
SMALL = {}
for _n, _w in (("a1", 12), ("a2", 12), ("a3", 12), ("m1", 12), ("m2", 12), ("zc", 12), ("zm", 12), ("cst", 8), ("wt", 8),
               ("bcol", 4), ("zo", 8), ("zp", 8), ("p16", 4), ("kcol", 4), ("vcol", 4), ("pmi", 16), ("jc", 16), ("tf", 16),
               ("rcum", 16), ("dp", 8), ("z", 16), ("bf", 12), ("hrow", 8), ("whi", 8), ("wlo", 8)):
    SMALL[_n] = (sum(w for o, w in SMALL.values()), _w)
SCRATCH = {"hland": ("dram", [12, 128, 1], "float32")}
for _t, _l in (("float32", "small=%d q0=128 qi=128 c2=128 sx=128 ones=128 neg=128 of=128 nul=128"
                % sum(w for o, w in SMALL.values())),
               ("bfloat16", "kb=64 hv=128 mc=256 mv=128 rsl=2048 hself=2 imod=128 cpat=128 onb=128 wh=8 l2=768 r1=768 r2=768"),
               ("bfloat16", "xin=2048 xs=2560 snd=3072 land=6144 yb=2048"),
               ("float16", "ha=128 hb2=128 oh=1024 prod=1024 tot=1 mb=128 hsel=2 hb=2 la=256 ra=2048 pc=128 rep=128"),
               ("int32", "kraw=64 kq=16 khi=16 klo=16 ti=16 thi=16 tlo=16 pci=16 pai=16 bq=6 bci=12"),
               ("uint16", "plist=128 wl=192 yoff=128 off=16")):
    for _b in _l.split():
        SCRATCH[_b.split("=")[0]] = ("sbuf", [128, int(_b.split("=")[1])], _t)
for _b, _w in (("kps", 1024), ("sps", 1024), ("tps", 512), ("hps", 512), ("pps", 512), ("sts", 512)):
    SCRATCH[_b] = ("psum", [128, _w], "float32")
SEMAPHORES = ["e%d" % i for i in range(NE)] + ["xa", "xl", "pa", "hd", "hc", "hr", "da", "yl", "sent"]
PLANS = {}


def plan(topo, cores):
    if "p" in PLANS:
        return PLANS["p"]
    rk = [topo.rack(topo.host(c)) for c in cores]
    p = {"partner": [], "twin": [], "help": [], "list": [],
         "rack": [[q for q in range(N) if rk[q] == rk[r]] for r in range(N)]}
    on_chip = [[k for k in range(512) if topo.host(k) == topo.host(c) and topo.chip(k) == topo.chip(c)] for c in cores]
    for r, c in enumerate(cores):
        s = [q for q in range(N) if rk[q] != rk[r] and topo.chip(cores[q]) == topo.chip(c) and topo.may_write(c, cores[q])][0]
        p["partner"].append(s)
        p["twin"].append([k for k in on_chip[s] if topo.die(k) != topo.die(cores[s]) and
                          all(topo.may_write(k, cores[q]) for q in p["rack"][s])][0])
    for r, c in enumerate(cores):
        pairs = zip(on_chip[r][::2], on_chip[r][1::2])
        h = [[k for k in two if k not in p["twin"] and topo.may_write(k, p["twin"][r])][-1] for two in pairs if c not in two]
        p["help"].append(h)
        p["list"].append([k for k in on_chip[r] if topo.die(k) == topo.die(c) and k != c and k not in h][0])
    PLANS["p"] = p
    return p


def engines(mask):
    return [1 << i for i in range(16) if mask >> i & 1]


def grp():
    return {"n": 0, "w": False, "sem": None, "cl": set(), "key": None}


def run(ops, qs, T):
    know, ns = {q: set() for q in qs}, 0
    for num, (q, f, kw, deps, G, n) in enumerate(ops):
        for d in deps:
            if isinstance(d, tuple):
                if d not in know[q]:
                    qs[q].wait_ge(T.sem[d[0]], d[1])
                    know[q].add(d)
            elif d["key"] not in know[q]:
                qs[q].wait_ge(T.sem["e%d" % d["sem"]], d["n"])
                know[q] |= d["cl"] | {d["key"]}
        if f is None:
            continue
        if G["key"] is None:
            G["key"] = num
            if G["w"]:
                G["sem"] = ns
                ns += 1
        G["cl"] |= know[q]
        i = f(**kw)
        if G["w"]:
            i.then_inc(T.sem["e%d" % G["sem"]], n)


def rank_program(g, core, T, topo):
    P = plan(topo, T.cores)
    r = T.rank_of(core)
    if r is not None:
        body(g, core, T, topo, P, r, "rank")
    elif core in P["twin"]:
        body(g, core, T, topo, P, P["twin"].index(core), "twin")
    else:
        for r in range(N):
            if core in P["help"][r] or core == P["list"][r]:
                body(g, core, T, topo, P, r, "list" if core == P["list"][r] else "help")


def body(g, core, T, topo, P, r, role):
    cores, partner, twin, lists_ = T.cores, P["partner"], P["twin"], P["list"]
    is_rank, is_list = role == "rank", role == "list"
    vec, act = g.vector, g.scalar
    home = partner[r] if role == "twin" else r
    mine = P["rack"][home]
    rtw = [twin[partner[s]] for s in mine]
    rli = [lists_[s] for s in mine]
    idx = mine.index(home)
    near = [cores[s] for s in mine if s != home]
    ops, sent = [], [0]

    def add(q, f, kw, deps=(), G=None, n=1):
        G = grp() if G is None else G
        G["n"] += n
        for d in deps:
            if not isinstance(d, tuple):
                d["w"] = True
        ops.append((q, f, kw, list(deps), G, n))
        return G

    def S(name, p0=0, p1=128, a=0, b=None):
        o, w = SMALL[name]
        return T.small[p0:p1, o + a:o + (w if b is None else b)]

    def ts(out, in0, s1, op0, deps, s2=None, op1=None, G=None):
        kw = dict(out=out, in0=in0, scalar1=s1, scalar2=s2, op0=op0)
        if op1 is not None:
            kw["op1"] = op1
        return add("v", vec.tensor_scalar, kw, deps, G)

    def tt(out, a, b, op, deps, G=None):
        return add("v", vec.tensor_tensor, dict(out=out, in0=a, in1=b, op=op), deps, G)

    def scan(out, d, deps, G=None, first=0.0):
        return add("v", vec.tensor_tensor_scan, dict(out=out, data0=d, data1=d, initial=first, op0=A.add, op1=A.max), deps, G)

    def fill(ap, c, G=None, deps=()):
        return add("v", vec.memset, dict(ap=ap, constant=c), deps, G)

    def cp(out, in_, deps, G=None, q="v"):
        if q == "v":
            return add("v", vec.tensor_copy, dict(out=out, in_=in_), deps, G)
        return add("s", act.activation, dict(out=out, in_=in_, func=F.Copy), deps, G)

    def mm(out, l, rh, start, stop, deps, G=None):
        return add("t", g.tensor.matmul, dict(out=out, lhsT=l, rhs=rh, start=start, stop=stop), deps, G)

    def iota(out, pat, base, cm, G=None, deps=(), small=True):
        kw = dict(out=out, pattern=pat, base=base, channel_multiplier=cm)
        if small:
            kw["allow_small_or_imprecise_dtypes"] = True
        return add("g", g.iota, kw, deps, G)

    def aff(out, in_, pat, op, fillv, base, cm, deps, G=None):
        return add("g", g.affine_select, dict(out=out, in_=in_, pattern=pat, compare_op=op, fill=fillv, base=base,
                                              channel_multiplier=cm), deps, G)

    def dma(q, out, in_, deps, G=None):
        return add(q, g.sync.dma_start if q == "y" else act.dma_start, dict(out=out, in_=in_), deps, G, 16)

    def remote(dst, out, in_, sem, mask, deps):
        rid, pid = topo.addr(dst, core)
        sent[0] += len(engines(mask))
        add("g", g.remote_dma, dict(out_ap=out, in_ap=in_, remote_sem=T.sem[sem], local_sem=T.sem.sent, pid=pid,
                                    routing_id=rid, dma_engine_mask=mask), deps)

    def fused(parts, deps):
        tr = []
        for dsts, sem, mask, src, dst in parts:
            ids = [DstId(rid=topo.addr(d, core)[0], pnc=topo.addr(d, core)[1]) for d in dsts]
            tr.append(RemoteDMATransfer(dst_ids=ids, dma_engine_mask=mask, remote_sem=T.sem[sem], srcs=[src], dsts=[dst] * len(ids)))
            sent[0] += len(engines(mask))
        add("g", g.remote_dma_fused, dict(transfers=tr, local_sem=T.sem.sent), deps)

    def blk(t, a, w=128):
        return t[:, a * w:(a + 1) * w]

    def finish():
        add("g", None, {}, [("sent", sent[0])])
        run(ops, {"g": g, "v": vec, "s": act, "y": g.sync, "t": g.tensor}, T)

    eng = engines(topo.mask(cores[r] if is_list else core, twin[r] if role == "help" else near[0]))
    half = len(eng) // 2
    lo, hi = eng[:half], sum(eng[half:])
    chipm = [e for e in engines(topo.mask(core, cores[home] if not is_rank else rtw[idx])) if e not in eng][:2 * half]

    if role == "help":
        part = blk(T.xin, P["help"][r].index(core), XP)
        remote(twin[r], part, part, "xa", sum(eng), [("xl", len(chipm))])
        finish()
        return

    gA, gH, gK, gM, gV, gC, gD, gE, gF, gG, gP, s0 = [grp() for _ in range(12)]
    a1, a2, a3, m1, m2 = [S(n, 0, 12) for n in ("a1", "a2", "a3", "m1", "m2")]

    def pats():
        iota(T.cpat[:], [[1, 128]], 0, 0, gC)
        iota(T.imod[:], [[0, 8], [1, 16]], 0, 0, gC)

    def gconst(on):
        iota(T.q0[:], [[16, 128]], 0, 0, gD)
        aff(S("rcum", 0, 12, 0, 13), T.ones[0:12, 0:13], [[1, 13]], A.is_gt, 0.0, 0, -1, [on], gE)
        iota(S("dp", 0, 64, 0, 6), [[W * (mine[1] - mine[0]), 6]], W * mine[0], 0, gE)

    def pmod():
        return ts(T.pai[:], T.pci[:], 15, A.bitwise_and, [gP])

    def qlist(pai):
        p16 = ts(S("p16", 0, 128, 0, 1), T.pai[:, 0:1], 0.0, A.add, [pai])
        return ts(T.qi[:], T.q0[:], S("p16", 0, 128, 0, 1), A.add, [gD, p16])

    def zeros():
        fill(T.sx[0:12, 0:1], 0.0, s0)
        fill(T.sx[0:12, 64:65], 0.0, s0)

    if is_rank:
        ftw, here = twin[r], rtw[idx]
        K, KQ, XG, RS = grp(), grp(), [grp() for _ in XC], grp()
        dma("y", T.kraw[0:16, :], T.key[:, 0:64], (), K)
        dma("s", T.kraw[16:32, :], T.key[:, 64:128], (), K)
        dma("y", T.kq[:], T.key[:], (), KQ)
        for h in range(4):
            dma("s", T.xin[:, XC[h][0]:XC[h][1]], T.x[:, XC[h][0]:XC[h][1]], (), XG[h])
        iota(S("pmi", 0, 32), [[-1, 16]], 0, 1, gA)
        for h in range(2):
            p0, p1 = 64 * h, 64 * h + 64
            iota(S("kcol", p0, p1, 0, 1), [[0, 1]], 0, 1, gK)
            iota(T.hself[p0:p1, :], [[2 * h - 1, 2]], 1 - h, 0, gV)
            iota(S("vcol", p0, p1, 0, 1), [[0, 1]], h, 2, gV)
        iota(T.pci[:], [[0, 16]], 0, 1, gP, [gK, gV], small=False)
        iota(T.mc[:], [[1, 16], [0, 16]], 0, 0, gM)
        iota(T.mv[:], [[1, 2], [2, 64]], 0, 0, gM)
        for h in range(2):
            fill(T.hv[0:32, 64 * h:64 * h + 64], 16.0 * h, gH)
        for i in range(16):
            ts(T.rsl[0:32, i * 128:(i + 1) * 128], T.hv[0:32, :], S("pmi", 0, 32, i, i + 1), A.is_equal, [gA, gH], G=RS)
        pai = pmod()
        off = cp(T.off[:], T.pai[:], [pai])
        for k, c in enumerate(P["help"][r]):
            remote(c, blk(T.xin, k, XP), blk(T.xin, k, XP), "xl", sum(chipm), [XG[k]])
        pats()
        iota(S("jc"), [[128, 8], [1024, 2]], 0, 1, gC)

        kcol = S("kcol", 0, 128, 0, 1)
        kb = cp(T.kb[0:32, :], T.kraw[0:32, :], [K])
        hk = ts(T.khi[:], T.kq[:], 3, A.arith_shift_right, [KQ])
        lk = ts(T.klo[:], T.kq[:], 7, A.bitwise_and, [KQ])
        ha = tt(T.ha[:], T.khi[:].indirect(T.off[:, 0:8]), T.mc[:, 0:128], A.is_equal, [hk, off, gM])
        hb2 = tt(T.hb2[:], T.klo[:].indirect(T.off[:, 0:8]), T.mc[:, 0:128], A.is_equal, [lk, off, gM])
        kp = [grp(), grp()]

        def spread(b):
            for i in range(16):
                mm(T.kps[:, 512 * b + i:512 * b + 512:16], T.rsl[0:32, i * 128:(i + 1) * 128], T.kb[0:32, 32 * b:32 * b + 32],
                   True, True, [RS, kb], kp[b])

        spread(0)
        hm = grp()
        for q in range(16):
            mm(T.hps[0:8, 0:8], T.ha[:, q:128:16], T.hb2[:, q:128:16], q == 0, q == 15, [ha, hb2], hm)
        spread(1)
        hr = cp(S("hrow", 0, 8), T.hps[0:8, 0:8], [hm], q="s")
        store = grp()
        for h in range(2):
            dma("ys"[h], T.hland[r, 64 * h:64 * h + 64, :], S("hrow", 0, 8), [hr], store)
        hl, ho = T.hland[r], T.hland[partner[r]]
        fused([([cores[partner[r]], ftw], "hc", lo[0], hl, hl), (near, "hd", lo[1], hl, hl), (rtw, "hd", lo[2], hl, hl),
               (rli, "hd", lo[3], hl, hl)], [store])
        xp = T.xin[:, XC[3][0]:XC[3][1]]
        remote(ftw, xp, xp, "xa", hi, [XG[3]])
        on = fill(T.ones[:], 1.0)
        hsel = cp(T.hsel[:], T.hself[:], [gV])
        mb = ts(T.mb[:], T.mv[:], S("vcol", 0, 128, 0, 1), A.is_gt, [gV, gM])
        gconst(on)
        oh, sc = [grp(), grp()], [grp(), grp()]
        for b in range(2):
            c0, c1 = 512 * b, 512 * b + 512
            ts(T.oh[:, c0:c1], T.kps[:, c0:c1], kcol, A.is_equal, [gK, kp[b]], G=oh[b])
            scan(T.sps[:, c0:c1], T.oh[:, c0:c1], [oh[b]] + sc[:b], sc[b], T.sps[:, c0 - 1:c0] if b else 0.0)
        fused([(near, "hr", lo[1], ho, ho), ([c for c in rtw if c != here], "hr", lo[2], ho, ho), (rli, "hr", lo[3], ho, ho)],
              [("hc", 1)])
        hdeps = [store, ("hc", 1), ("hd", 5), ("hr", 5)]
        tot = cp(T.tot[:], T.sps[:, 1023:1024], [sc[1]])
        bm = mm(T.sts[:, 0:1], T.mb[:], T.tot[:], True, True, [tot, mb])
        tm = grp()
        for c in range(4):
            cols = slice(256 * c, 256 * c + 256)
            pr = tt(T.prod[:, cols], T.oh[:, cols], T.sps[:, cols], A.mult, sc)
            if c == 0:
                hb = ts(T.hb[:], T.hsel[:], T.sts[:, 0:1], A.mult, [hsel, bm])
            for q in (2 * c, 2 * c + 1):
                mm(blk(T.tps, q, 2), blk(T.prod, q), T.hsel[:], True, False, [pr, hsel], tm)
                mm(blk(T.tps, q, 2), blk(T.oh, q), T.hb[:], False, True, [hb], tm)
        rep = ts(T.rep[0:16, :], T.imod[0:16, :], S("kcol", 0, 16, 0, 1), A.is_equal, [gC, gK])
        tail = fill(T.xs[:, W:W + CAP], 0.0)
        ti = ts(T.ti[:], T.tps[:, 0:16], 1.0, A.subtract, [tm])
        th = ts(T.thi[:], T.ti[:], 4, A.arith_shift_right, [ti])
        tl = ts(T.tlo[:], T.ti[:], 15, A.bitwise_and, [ti])
        tf = cp(S("tf"), T.thi[:], [th])
        la = tt(T.la[:], T.tlo[:].indirect(T.off[:]), T.mc[:], A.is_equal, [tl, off, gM])
        pm = grp()
        for a in range(16):
            if a % 2 == 0:
                og = grp()
            ts(blk(T.ra, a), T.cpat[:], S("tf", 0, 128, a, a + 1), A.is_equal, [tf, gC], S("jc", 0, 128, a, a + 1), A.mult, og)
            if a % 2 == 1:
                for b in (a - 1, a):
                    mm(T.tps[0:16, 0:128], T.la[:, b:256:16], blk(T.ra, b), b == 0, b == 15, [la, og], pm)
        pc = cp(T.pc[0:16, :], T.tps[0:16, 0:128], [pm])
        pr = mm(T.sps[:, 0:128], T.rep[0:16, :], T.pc[0:16, :], True, True, [pc, rep])
        pl = cp(T.plist[:], T.sps[:, 0:128], [pr])
        remote(ftw, T.plist[:], T.plist[:], "pa", sum(lo), [pl])
        xdeps = [pl] + XG
    else:
        on = fill(T.ones[:], 1.0)
        zeros()
        iota(T.pci[:], [[0, 16]], 0, 1, gP, small=False)
        gconst(on)
        pai = pmod()
        qi = qlist(pai)
        if is_list:
            pats()
            aff(a1, T.ones[0:12, 0:12], [[-1, 12]], A.is_equal, 0.0, 0, 1, [on], gF)
            aff(a2, T.ones[0:12, 0:12], [[-1, 12]], A.is_equal, 0.0, 1, 1, [on], gG)
            aff(a3, a2, [[100, 12]], A.not_equal, 1.0, -11, 1, [gG], gF)
            g1 = tt(m1, a1, a3, A.subtract, [gF])
            g2 = ts(m2, a2, -1.0, A.mult, [gG])
            ng = fill(T.neg[:], -1.0)
            cs = fill(S("cst"), 512.0)
            cs2 = fill(S("cst", 0, 64, 0, 1), -512.0 * 11, deps=[cs])
            onb, nul = fill(T.onb[:], 1.0), grp()
            fill(T.of[:], 0.0, nul)
            fill(T.nul[:], 0.0, nul)
            hdeps = [("hd", 6), ("hr", 6)]
        else:
            tail = fill(T.xs[:, W:W + CAP], 0.0)
            hdeps = [("hc", 1), ("hd", 6), ("hr", 5)]
            xdeps = [("xa", 3 * len(eng) + half), ("pa", half)]

    XS = grp()

    def lsort(pieces):
        for q, a, b in pieces:
            cp(T.xs[:, a:b], T.xin[:].indirect(T.plist[:, a // 16:b // 16]), xdeps, XS, q)

    if is_rank:
        lsort((("s", H, W), ("v", 0, 512)))
        zeros()

    ld = dma("y", T.c2[0:12, :], T.hland[:], hdeps)
    sx = grp()
    for b in (0, 64):
        scan(T.sx[0:12, b + 1:b + 64], T.c2[0:12, b:b + 63], [ld], sx)
    rc, o13 = S("rcum", 0, 12, 0, 13), T.ones[0:12, 0:13]
    mm(T.pps[:, 0:13], T.c2[0:12, :], rc, True, False, [ld, gE])
    pp = mm(T.pps[:, 0:13], T.sx[0:12, :], o13, False, True, [sx, s0, on])

    if not is_list:
        if is_rank:
            lsort((("v", 512, 768),))
            qi = qlist(pai)
        zo = ts(S("zo", 0, 64, 0, 6), S("dp", 0, 64, 0, 6), T.pps[0:64, r + 1:r + 2], A.min, [pp, gE], T.pps[0:64, r:r + 1], A.max)
        zp = ts(S("zp", 0, 64, 0, 6), S("zo", 0, 64, 0, 6), T.pps[0:64, r:r + 1], A.subtract, [zo])
        st = mm(T.sts[:, 0:6], T.ones[0:64, :], S("zp", 0, 64, 0, 6), True, True, [zp, on])
        if is_rank:
            lsort((("v", 768, H),))

        order = [mine[(idx + 1 + k) % 6] for k in range(6)]
        slot = blk(T.land, r, CAP)
        wls, wins = {}, [grp() for _ in range(6)]

        def wlist(k):
            e = mine.index(order[k])
            wls[k] = ts(blk(T.wl, k, 32), T.qi[:, 0:32], T.sts[:, e:e + 1], A.add, [st, qi])

        def window(k, q, a=0, b=CAP):
            base, t = (CAP * r, T.land) if order[k] == r else (CAP * k, T.snd)
            cp(t[:, base + a:base + b], T.xs[:].indirect(T.wl[:, 32 * k + a // 16:32 * k + b // 16]), [wls[k], XS, tail], wins[k], q)

        if not is_rank:
            for k in range(6):
                wlist(k)
            lsort((("v", 0, H), ("s", H, W)))
        for k, lists in ((0, (0,)), (1, (2, 1)), (3, (4, 3)), (5, (5,))):
            if is_rank:
                for m in lists:
                    wlist(m)
            if k in (0, 5):
                window(k, "v", 0, 256)
                window(k, "s", 256, 512)
            else:
                window(k, "v")
                window(k + 1, "s")
        remote(cores[order[0]], slot, blk(T.snd, 0, CAP), "da", sum(eng), [wins[0]])
        p = [([cores[order[k]]], "da", sum(lo) if k % 2 else hi, blk(T.snd, k, CAP), slot) for k in range(1, 5)]
        fused(p[:2], wins[1:3])
        if is_rank:
            fused(p[2:], wins[3:5])
        else:
            fused(p[2:] + [([cores[home]], "da", sum(chipm[:half]), blk(T.snd, 5, CAP), slot)], wins[3:6])
    else:
        dl, bq, bc, wt, dm = [grp() for _ in range(5)]
        zc, zm, z = S("zc", 0, 64), S("zm", 0, 64), T.pps[0:64, 0:12]
        Y0 = float(W * r)
        z1 = ts(zc, z, Y0, A.max, [pp])
        z2 = tt(zm, zc, T.pps[0:64, 1:13], A.min, [z1])
        zz = tt(S("z", 0, 64, 1, 13), zm, z, A.subtract, [z2])
        zw = ts(S("z", 0, 64, 0, 1), S("z", 0, 64, 12, 13), 0.0, A.add, [zz])
        mm(T.hps[:, 0:12], T.sx[0:12, :], m1, True, False, [g1, sx, s0], dl)
        mm(T.hps[:, 0:12], T.c2[0:12, :], m2, False, False, [g2, ld], dl)
        mm(T.hps[:, 0:12], T.neg[0:64, :], S("z", 0, 64, 1, 13), False, False, [ng, zz], dl)
        mm(T.hps[:, 0:12], T.ones[0:64, :], S("z", 0, 64, 0, 12), False, True, [zz, zw], dl)
        mm(T.hps[:, 12:13], T.neg[0:64, :], S("z", 0, 64, 12, 13), True, True, [zz], dl)
        for h in range(2):
            p0, p1 = 64 * h, 64 * h + 64
            ts(T.bq[p0:p1, :], T.pps[p0:p1, h:12:2], Y0, A.subtract, [pp], 0.0, A.max, bq)
        ts(T.bci[:, 0:6], T.bq[:], 4, A.arith_shift_right, [bq], G=bc)
        ts(T.bci[:, 6:12], T.bq[:], 15, A.bitwise_and, [bq], G=bc)
        bf = cp(S("bf"), T.bci[:], [bc])
        for h in range(2):
            p0, p1 = 64 * h, 64 * h + 64
            tt(S("wt", p0, p1, 0, 6), T.hps[p0:p1, h:12:2], S("cst", p0, p1, 0, 6), A.add, [dl, cs, cs2], wt)
        bcol = ts(S("bcol", 0, 128, 0, 1), T.hps[:, 12:13], Y0 + 512.0 * 11, A.add, [dl])
        wr = cp(T.wh[:, 0:6], S("wt", 0, 128, 0, 6), [wt])
        wh = cp(S("whi", 0, 128, 0, 6), T.wh[:, 0:6], [wr])
        wl = tt(S("wlo", 0, 128, 0, 6), S("wt", 0, 128, 0, 6), T.wh[:, 0:6], A.subtract, [wt, wr])
        for q in range(6):
            og = grp()
            bc_, bi_ = S("bf", 0, 128, q, q + 1), S("bf", 0, 128, 6 + q, 7 + q)
            ts(blk(T.l2, q), T.imod[:], bi_, A.is_ge, [bf, gC], G=og)
            ts(blk(T.r1, q), T.cpat[:], bc_, A.is_equal, [bf, wh, gC], S("whi", 0, 128, q, q + 1), A.mult, og)
            ts(blk(T.r2, q), T.cpat[:], bc_, A.is_equal, [bf, wl, gC], S("wlo", 0, 128, q, q + 1), A.mult, og)
            for k, rr in enumerate((T.r1, T.r2)):
                first, last = (q, k) == (0, 0), (q, k) == (5, 1)
                mm(T.kps[:, 512:640], T.onb[:], blk(rr, q), first, last, [og, onb], dm)
                mm(T.sps[:, 512:640], blk(T.l2, q), blk(rr, q), first, last, [og], dm)
        of = add("v", vec.tensor_tensor_scan, dict(out=T.of[:, 1:128], data0=T.kps[:, 512:639], data1=T.nul[:, 0:127],
                                                   initial=0.0, op0=A.add, op1=A.add), [dm, nul])
        of2 = tt(T.of[:], T.of[:], T.sps[:, 512:640], A.add, [of])
        of3 = tt(T.of[:], T.of[:], T.qi[:], A.add, [of2, qi])
        yo = ts(T.yoff[:], T.of[:], S("bcol", 0, 128, 0, 1), A.add, [of3, bcol])
        remote(cores[r], T.yoff[:], T.yoff[:], "yl", sum(chipm[:half]), [yo])

    if is_rank:
        stores = grp()
        nd = sum(len(eng) if mine[(i + 1) % 6] == home else half for i in range(6) if i != idx) * 2 + half
        for k, (a, b) in enumerate(YC):
            w = cp(T.yb[:, a:b], T.land[:].indirect(T.yoff[:, a // 16:b // 16]), [wins[5], ("yl", half), ("da", nd)], q="vs"[k % 2])
            dma("y", T.y[:, a:b], T.yb[:, a:b], [w], stores)
        add("y", None, {}, [stores])
    finish()
